import numpy as np
import ml_dtypes


def mxq(x, axis, fmt="e4m3"):
    dtype, down = {"e4m3": (ml_dtypes.float8_e4m3fn, 7), "e5m2": (ml_dtypes.float8_e5m2, 14)}[fmt]
    v = np.moveaxis(np.asarray(x, np.float32).astype(ml_dtypes.bfloat16).astype(np.float64), axis, -1)
    blocks = v.reshape(v.shape[:-1] + (-1, 32))
    amax = np.abs(blocks).max(-1, keepdims=True)
    byte = np.maximum(np.where(amax > 0, np.frexp(amax)[1] - 1 + 127, 0) - down, 1)
    scale = np.exp2(byte - 127.0)
    codes = (blocks / scale).astype(np.float32).astype(dtype).astype(np.float64)
    return np.moveaxis((codes * scale).reshape(v.shape), -1, axis)


WIDE = False


def mx_kscale(k):
    if not WIDE:
        return np.ones(k)
    levels = np.array([10, -10, 5, -5, 0])
    if k % 512:
        return np.exp2(np.random.permutation(np.resize(levels, k // 32))).repeat(32)
    a = np.empty((k // 512, 16))
    for p in range(k // 512):
        a[p, :8] = np.random.permutation(np.resize(levels, 8))
        for g in range(8):
            far = levels[np.abs(levels - a[p, g]) >= 10]
            a[p, g + 8] = far[np.random.randint(len(far))]
    return np.exp2(a.ravel()).repeat(32)


def f64(x):
    return np.asarray(x).astype(np.float64)


def striped(idx):
    return np.tile(idx.reshape(-1, 16).T, (8, 1)).astype(np.uint16)


def unstriped(offs):
    return offs[:16].T.reshape(-1).astype(np.int64)


def pack_weight(w):
    k, n = w.shape
    w = f64(np.asarray(w, np.float32).astype(ml_dtypes.bfloat16)).reshape(k // 32, 32, n)
    amax = np.abs(w).max(1)
    byte = np.clip(np.where(amax > 0, np.frexp(amax)[1] - 1 + 127 - 7, 1), 1, 254)
    scaled = (w * np.exp2(127.0 - byte)[:, None, :]).reshape(k, n).astype(np.float32)
    words = np.ascontiguousarray(scaled.reshape(k // 512, 128, 4, n).transpose(0, 1, 3, 2)).astype(ml_dtypes.float8_e4m3fn).view(np.uint8)
    return words, np.ascontiguousarray(byte.astype(np.uint8).reshape(k // 512, 16, n))


def unpack_weight(words, scales):
    g, p, n, _ = words.shape
    vals = np.ascontiguousarray(words).view(ml_dtypes.float8_e4m3fn).astype(np.float64) * np.repeat(np.exp2(scales.astype(np.float64) - 127.0), 8, axis=1)[..., None]
    return vals.transpose(0, 1, 3, 2).reshape(g * 512, n)


K, T, S, H, V, W = 512, 2048, 512, 512, 512, 2048
P = 2 ** 7


def setup_inputs():
    n = np.random.standard_normal
    s = mx_kscale(K)[:, None]
    u = mx_kscale(H)
    packed_xT = pack_weight(n((K, T)) * s)
    packed_eT = pack_weight(n((H, W)) / np.sqrt(H) / u[:, None])
    return {
        "x_words": packed_xT[0],
        "x_scales": packed_xT[1],
        "w1": (n((K, H)) / np.sqrt(K) / s * u).astype(np.float32),
        "e_words": packed_eT[0],
        "e_scales": packed_eT[1],
        "qn": (np.tile(np.random.uniform(1.5, 2.5, W), (P, 1))).astype(np.float32),
        "own": (np.random.uniform(1.5, 2.5, (S, 1))).astype(np.float32),
        "act": (np.tile(n(W), (P, 1))).astype(np.float32),
        "offs": striped(np.random.permutation(T)[:S]),
        "refs": striped(np.random.permutation(W)[:V]),
    }


def reference(x_words, x_scales, w1, e_words, e_scales, qn, own, act, offs, refs):
    xq = unpack_weight(x_words, x_scales)[:, unstriped(offs)]
    h = mxq(f64(w1), 0, "e4m3").T @ xq
    e_refs = unpack_weight(e_words, e_scales)[:, unstriped(refs)]
    y = 0.3 * ((mxq(h, 0, "e4m3").T @ e_refs))
    dd = f64(qn)[:1][:, unstriped(refs)] - y + f64(own)
    z = y / dd
    return np.tanh(z * (f64(act)[:1][:, unstriped(refs)]))

@@ -1,0 +1,179 @@
+from contextlib import ExitStack
+
+import concourse.mybir as mybir
+from concourse.masks import make_identity
+
+K, T, S, H, V, W = 512, 2048, 512, 512, 512, 2048
+FLOPS = 2 * K * H * S + 2 * H * S * V
+BYTES = K * T + K * T // 32 + H * W + H * W // 32 + 4 * K * H + 2 * 4 * W + 4 * S + 2 * 2 * 128 * 32 + 4 * S * V
+
+F32 = mybir.dt.float32
+BF16 = mybir.dt.bfloat16
+I32 = mybir.dt.int32
+U32 = mybir.dt.uint32
+U16 = mybir.dt.uint16
+U8 = mybir.dt.uint8
+FP8X4 = mybir.dt.float8_e4m3fn_x4
+ACT = mybir.ActivationFunctionType
+ALU = mybir.AluOpType
+
+P = 128
+PACK = 4
+NB = 4
+Y_SCALE = 0.3
+ACT_ROW = 64
+
+
+def load_scale_rows(queue, plane, rows):
+    for q in range(4):
+        queue.dma_start(out=plane[32 * q : 32 * q + 4, :].bitcast(I32), in_=rows[0, 4 * q : 4 * q + 4, :].bitcast(I32))
+
+
+def tile_picked_ytani_act_p_kernel(
+    tc, x_words, x_scales, w1, e_words, e_scales, qn, own, act, offs, refs, out
+):
+    nc = tc.nc
+    with ExitStack() as ctx:
+        keep = ctx.enter_context(tc.tile_pool(name="keep", bufs=1))
+        psum = ctx.enter_context(tc.psum_pool(name="psum", bufs=1))
+
+        offs_sb = keep.tile([P, S // 16], U16, name="offs_sb")
+        refs_sb = keep.tile([P, V // 16], U16, name="refs_sb")
+        xs_tab = keep.tile([P, T], U8, name="xs_tab", tag="xs_then_ew", align_bytes=64)
+        es_tab = keep.tile([P, W], U8, name="es_tab", align_bytes=64)
+        qa_tab = keep.tile([P, W], F32, name="qa_tab", align_bytes=64)
+        w_raw = [keep.tile([P, PACK, H // 2], F32, name="w_raw%d" % u, align_bytes=64) for u in range(2)]
+        own_col = keep.tile([P, NB], F32, name="own_col")
+        ident = keep.tile([P, P], F32, name="ident", align_bytes=64)
+        warm_in = keep.tile([P, 1], F32, name="warm_in", tag="warm_then_xw", align_bytes=64)
+        warm_out = keep.tile([P, 1], F32, name="warm_out")
+
+        nc.vector.memset(xs_tab[:].bitcast(I32), 0)
+        nc.vector.memset(warm_in[:], 1.0)
+        nc.vector.memset(es_tab[:].bitcast(I32), 0)
+        nc.vector.memset(qa_tab[:], 0.0)
+
+        w_rows = w1.rearrange("(p r) c -> p r c", r=PACK)
+        nc.sync.dma_start(offs_sb[:], offs)
+        nc.sync.dma_start(refs_sb[:], refs)
+        for u in range(2):
+            nc.sync.dma_start(out=w_raw[u][:], in_=w_rows[:, :, u * (H // 2) : (u + 1) * (H // 2)])
+        load_scale_rows(nc.scalar, xs_tab, x_scales)
+        nc.scalar.activation(warm_out[:], warm_in[:], ACT.Abs_reciprocal_sqrt)
+        nc.scalar.dma_start(out=qa_tab[0:1, :], in_=qn[0:1, :])
+        nc.scalar.dma_start(out=qa_tab[ACT_ROW : ACT_ROW + 1, :], in_=act[0:1, :])
+        xw_tab = keep.tile([P, T], U32, name="xw_tab", tag="warm_then_xw", align_bytes=64)
+        nc.sync.dma_start(out=xw_tab[:].bitcast(I32), in_=x_words[0].rearrange("p n t -> p (n t)").bitcast(I32))
+        nc.gpsimd.dma_start(out=own_col[:], in_=own.rearrange("(p c) o -> p (c o)", c=NB))
+        load_scale_rows(nc.gpsimd, es_tab, e_scales)
+        make_identity(nc, ident[:])
+
+        w_bf = keep.tile([P, PACK, P, PACK], BF16, name="w_bf", tag="w_then_es", align_bytes=64)
+        for u in range(2):
+            nc.scalar.copy(
+                out=w_bf[:, :, u * (P // 2) : (u + 1) * (P // 2), :].rearrange("p j m r -> p m j r"),
+                in_=w_raw[u][:].rearrange("p r (m j) -> p m j r", j=PACK),
+            )
+
+        xs = keep.tile([P, S], U8, name="xs", align_bytes=64)
+        nc.vector.tensor_copy(xs[:], xs_tab[:].indirect(offs_sb[:]))
+        ew_tab = keep.tile([P, W], U32, name="ew_tab", tag="xs_then_ew", align_bytes=64)
+        nc.sync.dma_start(out=ew_tab[:].bitcast(I32), in_=e_words[0].rearrange("p n t -> p (n t)").bitcast(I32))
+        qa = keep.tile([P, V], F32, name="qa", align_bytes=64)
+        nc.vector.tensor_copy(qa[:], qa_tab[:].indirect(refs_sb[:]))
+
+        own_ps = psum.tile([P, NB, P], F32, name="own_ps", tag="s0")
+        for c in range(NB):
+            nc.tensor.transpose(own_ps[:, c, :], own_col[:, c : c + 1].to_broadcast([P, P]), ident[:])
+        own_row = keep.tile([P, S], F32, name="own_row", align_bytes=64)
+        nc.scalar.activation(
+            own_row[:].rearrange("p (n c) -> p n c", c=NB), own_ps[:].rearrange("p c n -> p n c"), ACT.Copy, scale=1.0 / Y_SCALE
+        )
+        qa_ps = psum.tile([P, NB, P], F32, name="qa_ps", tag="s1")
+        for b in range(NB):
+            nc.tensor.transpose(qa_ps[:, b, :], qa[:, b * P : (b + 1) * P], ident[:])
+        qa_col = keep.tile([P, NB, 2], F32, name="qa_col")
+        nc.scalar.activation(qa_col[:], qa_ps[:, :, 0:P:ACT_ROW], ACT.Copy, scale=1.0 / Y_SCALE)
+
+        wq = keep.tile([P, H], U32, name="wq", align_bytes=64)
+        ws = keep.tile([P, H], U8, name="ws", align_bytes=64)
+        nc.vector.quantize_mx(out=wq[:].bitcast(FP8X4), scales=ws[:], in_=w_bf[:].rearrange("p j m r -> p (j m r)"))
+
+        xq = [keep.tile([P, S // 2], U32, name="xq%d" % u, align_bytes=64) for u in range(2)]
+        for u in range(2):
+            nc.vector.tensor_copy(xq[u][:], xw_tab[:].indirect(offs_sb[:, 16 * u : 16 * (u + 1)]))
+        es = keep.tile([P, V], U8, name="es", tag="w_then_es", align_bytes=64)
+        nc.vector.tensor_copy(es[:], es_tab[:].indirect(refs_sb[:]))
+
+        hq = keep.tile([P, S], U32, name="hq", align_bytes=64)
+        hs = keep.tile([P, S], U8, name="hs", align_bytes=64)
+        h_bf = []
+        for c in range(NB):
+            h_ps = psum.tile([P, PACK, P], F32, name="h_ps%d" % c, tag="h%d" % c)
+            cols = slice((c % 2) * P, (c % 2 + 1) * P)
+            for j in range(PACK):
+                nc.tensor.matmul_mx(
+                    out=h_ps[:, j, :],
+                    lhsT=wq[:, j * P : (j + 1) * P].bitcast(FP8X4),
+                    lhsT_scale=ws[:, j * P : (j + 1) * P],
+                    rhs=xq[c // 2][:, cols].bitcast(FP8X4),
+                    rhs_scale=xs[:, c * P : (c + 1) * P],
+                    start=True,
+                    stop=True,
+                )
+            hb = keep.tile([P, P, PACK], BF16, name="h_bf%d" % c, align_bytes=64)
+            nc.scalar.copy(out=hb[:], in_=h_ps[:].rearrange("p j n -> p n j"))
+            h_bf.append(hb)
+
+        eq = [keep.tile([P, V // 2], U32, name="eq%d" % u, align_bytes=64) for u in range(2)]
+        for c in range(NB):
+            nc.vector.quantize_mx(
+                out=hq[:, c * P : (c + 1) * P].bitcast(FP8X4),
+                scales=hs[:, c * P : (c + 1) * P],
+                in_=h_bf[c][:].rearrange("p n j -> p (n j)"),
+            )
+            if c % 2 == 0:
+                u = c // 2
+                nc.vector.tensor_copy(eq[u][:], ew_tab[:].indirect(refs_sb[:, 16 * u : 16 * (u + 1)]))
+
+        s_ps, dneg, root, inv, sgn, num, arg = [], [], [], [], [], [], []
+        for b in range(NB):
+            sp = psum.tile([P, S], F32, name="s_ps%d" % b, tag="s%d" % b)
+            cols = slice((b % 2) * P, (b % 2 + 1) * P)
+            nc.tensor.matmul_mx(
+                out=sp[:],
+                lhsT=eq[b // 2][:, cols].bitcast(FP8X4),
+                lhsT_scale=es[:, b * P : (b + 1) * P],
+                rhs=hq[:].bitcast(FP8X4),
+                rhs_scale=hs[:],
+                start=True,
+                stop=True,
+            )
+            s_ps.append(sp)
+            for group, label in ((dneg, "dneg"), (root, "root"), (inv, "inv"), (sgn, "sgn"), (num, "num"), (arg, "arg")):
+                group.append(keep.tile([P, S], F32, name="%s%d" % (label, b), align_bytes=64))
+
+        for b in range(NB):
+            nc.vector.scalar_tensor_tensor(dneg[b][:], s_ps[b][:], qa_col[:, b, 0:1], own_row[:], ALU.subtract, ALU.subtract)
+            nc.scalar.activation(root[b][:], dneg[b][:], ACT.Abs_reciprocal_sqrt)
+        for b in range(NB):
+            nc.vector.tensor_scalar(sgn[b][:], dneg[b][:], 0.0, 0.5, ALU.is_gt, ALU.subtract)
+            nc.scalar.activation(inv[b][:], root[b][:], ACT.Square)
+
+        def scale_sums(b):
+            nc.vector.scalar_tensor_tensor(num[b][:], s_ps[b][:], qa_col[:, b, 1:2], inv[b][:], ALU.mult, ALU.mult)
+
+        def finish(b):
+            nc.vector.tensor_tensor(arg[b][:], num[b][:], sgn[b][:], ALU.mult)
+            o_ps = psum.tile([P, NB, P], F32, name="o_ps%d" % b, tag="h%d" % b)
+            for c in range(NB):
+                nc.tensor.transpose(o_ps[:, c, :], arg[b][:, c * P : (c + 1) * P], ident[:])
+            res = keep.tile([P, NB, P], F32, name="res%d" % b, align_bytes=64)
+            nc.scalar.activation(res[:], o_ps[:], ACT.Tanh, scale=-2.0 * Y_SCALE)
+            nc.sync.dma_start(out=out[:, b * P : (b + 1) * P].rearrange("(c p) v -> p c v", p=P), in_=res[:])
+
+        scale_sums(0)
+        for b in range(1, NB):
+            scale_sums(b)
+            finish(b - 1)
+        finish(NB - 1)

@@ -20,12 +20,13 @@ ALU = mybir.AluOpType
 P = 128
 PACK = 4
 NB = 4
+HALF = 256
 Y_SCALE = 0.3
 ACT_ROW = 64
 
 
-def load_scale_rows(queue, plane, rows):
-    for q in range(4):
+def load_scale_rows(queues, plane, rows):
+    for q, queue in enumerate(queues):
         queue.dma_start(out=plane[32 * q : 32 * q + 4, :].bitcast(I32), in_=rows[0, 4 * q : 4 * q + 4, :].bitcast(I32))
 
 
@@ -39,48 +40,55 @@ def tile_picked_ytani_act_p_kernel(
 
         offs_sb = keep.tile([P, S // 16], U16, name="offs_sb")
         refs_sb = keep.tile([P, V // 16], U16, name="refs_sb")
-        xs_tab = keep.tile([P, T], U8, name="xs_tab", tag="xs_then_ew", align_bytes=64)
-        es_tab = keep.tile([P, W], U8, name="es_tab", align_bytes=64)
-        qa_tab = keep.tile([P, W], F32, name="qa_tab", align_bytes=64)
-        w_raw = [keep.tile([P, PACK, H // 2], F32, name="w_raw%d" % u, align_bytes=64) for u in range(2)]
+        xs_tab = keep.tile([P, T], U8, name="xs_tab", align_bytes=64)
+        es_tab = keep.tile([P, W], U8, name="es_tab", tag="es_then_hq", align_bytes=64)
+        qa_tab = keep.tile([P, W], F32, name="qa_tab", tag="qa_then_eq", align_bytes=64)
+        xw_tab = keep.tile([P, T], U32, name="xw_tab", tag="xw_then_qa", align_bytes=64)
+        ew_tab = keep.tile([P, W], U32, name="ew_tab", tag="ew_then_es", align_bytes=64)
+        w_raw = keep.tile([P, PACK, H], F32, name="w_raw", align_bytes=64)
         own_col = keep.tile([P, NB], F32, name="own_col")
         ident = keep.tile([P, P], F32, name="ident", align_bytes=64)
-        warm_in = keep.tile([P, 1], F32, name="warm_in", tag="warm_then_xw", align_bytes=64)
+        warm_in = keep.tile([P, 1], F32, name="warm_in")
         warm_out = keep.tile([P, 1], F32, name="warm_out")
 
-        nc.vector.memset(xs_tab[:].bitcast(I32), 0)
+        nc.gpsimd.memset(xs_tab[:].bitcast(I32), 0)
+        nc.gpsimd.memset(qa_tab[:, : W // 2], 0.0)
+        nc.vector.memset(qa_tab[:, W // 2 :], 0.0)
         nc.vector.memset(warm_in[:], 1.0)
         nc.vector.memset(es_tab[:].bitcast(I32), 0)
-        nc.vector.memset(qa_tab[:], 0.0)
 
-        w_rows = w1.rearrange("(p r) c -> p r c", r=PACK)
         nc.sync.dma_start(offs_sb[:], offs)
         nc.sync.dma_start(refs_sb[:], refs)
-        for u in range(2):
-            nc.sync.dma_start(out=w_raw[u][:], in_=w_rows[:, :, u * (H // 2) : (u + 1) * (H // 2)])
-        load_scale_rows(nc.scalar, xs_tab, x_scales)
-        nc.scalar.activation(warm_out[:], warm_in[:], ACT.Abs_reciprocal_sqrt)
-        nc.scalar.dma_start(out=qa_tab[0:1, :], in_=qn[0:1, :])
-        nc.scalar.dma_start(out=qa_tab[ACT_ROW : ACT_ROW + 1, :], in_=act[0:1, :])
-        xw_tab = keep.tile([P, T], U32, name="xw_tab", tag="warm_then_xw", align_bytes=64)
+        load_scale_rows((nc.sync, nc.sync, nc.scalar, nc.scalar), xs_tab, x_scales)
+        nc.sync.dma_start(out=w_raw[:], in_=w1.rearrange("(p r) c -> p r c", r=PACK))
         nc.sync.dma_start(out=xw_tab[:].bitcast(I32), in_=x_words[0].rearrange("p n t -> p (n t)").bitcast(I32))
-        nc.gpsimd.dma_start(out=own_col[:], in_=own.rearrange("(p c) o -> p (c o)", c=NB))
-        load_scale_rows(nc.gpsimd, es_tab, e_scales)
+        nc.sync.dma_start(out=qa_tab[0:1, :], in_=qn[0:1, :])
+        nc.sync.dma_start(out=qa_tab[ACT_ROW : ACT_ROW + 1, :], in_=act[0:1, :])
+        nc.sync.dma_start(out=ew_tab[:].bitcast(I32), in_=e_words[0].rearrange("p n t -> p (n t)").bitcast(I32))
+        load_scale_rows((nc.sync,) * 4, es_tab, e_scales)
+        nc.scalar.dma_start(out=own_col[:], in_=own.rearrange("(p c) o -> p (c o)", c=NB))
+        nc.scalar.activation(warm_out[:], warm_in[:], ACT.Abs_reciprocal_sqrt)
         make_identity(nc, ident[:])
-
-        w_bf = keep.tile([P, PACK, P, PACK], BF16, name="w_bf", tag="w_then_es", align_bytes=64)
-        for u in range(2):
-            nc.scalar.copy(
-                out=w_bf[:, :, u * (P // 2) : (u + 1) * (P // 2), :].rearrange("p j m r -> p m j r"),
-                in_=w_raw[u][:].rearrange("p r (m j) -> p m j r", j=PACK),
-            )
 
         xs = keep.tile([P, S], U8, name="xs", align_bytes=64)
         nc.vector.tensor_copy(xs[:], xs_tab[:].indirect(offs_sb[:]))
-        ew_tab = keep.tile([P, W], U32, name="ew_tab", tag="xs_then_ew", align_bytes=64)
-        nc.sync.dma_start(out=ew_tab[:].bitcast(I32), in_=e_words[0].rearrange("p n t -> p (n t)").bitcast(I32))
-        qa = keep.tile([P, V], F32, name="qa", align_bytes=64)
-        nc.vector.tensor_copy(qa[:], qa_tab[:].indirect(refs_sb[:]))
+
+        w_view = w_raw[:].rearrange("p r (m j) -> p m j r", j=PACK)
+        w_bf = [
+            keep.tile([P, 2, P, PACK], BF16, name="w_bf0", tag="w_then_xq", align_bytes=64),
+            keep.tile([P, 2, P, PACK], BF16, name="w_bf1", align_bytes=64),
+        ]
+        nc.scalar.copy(out=w_bf[0][:].rearrange("p j m r -> p m j r"), in_=w_view[:, :, 0:2, :])
+        nc.vector.tensor_copy(out=w_bf[1][:].rearrange("p j m r -> p m j r"), in_=w_view[:, :, 2:4, :])
+
+        wq = keep.tile([P, H], U32, name="wq", align_bytes=64)
+        ws = keep.tile([P, H], U8, name="ws", align_bytes=64)
+        for a in (1, 0):
+            nc.vector.quantize_mx(
+                out=wq[:, a * HALF : (a + 1) * HALF].bitcast(FP8X4),
+                scales=ws[:, a * HALF : (a + 1) * HALF],
+                in_=w_bf[a][:].rearrange("p j m r -> p (j m r)"),
+            )
 
         own_ps = psum.tile([P, NB, P], F32, name="own_ps", tag="s0")
         for c in range(NB):
@@ -89,25 +97,20 @@ def tile_picked_ytani_act_p_kernel(
         nc.scalar.activation(
             own_row[:].rearrange("p (n c) -> p n c", c=NB), own_ps[:].rearrange("p c n -> p n c"), ACT.Copy, scale=1.0 / Y_SCALE
         )
-        qa_ps = psum.tile([P, NB, P], F32, name="qa_ps", tag="s1")
-        for b in range(NB):
-            nc.tensor.transpose(qa_ps[:, b, :], qa[:, b * P : (b + 1) * P], ident[:])
-        qa_col = keep.tile([P, NB, 2], F32, name="qa_col")
-        nc.scalar.activation(qa_col[:], qa_ps[:, :, 0:P:ACT_ROW], ACT.Copy, scale=1.0 / Y_SCALE)
 
-        wq = keep.tile([P, H], U32, name="wq", align_bytes=64)
-        ws = keep.tile([P, H], U8, name="ws", align_bytes=64)
-        nc.vector.quantize_mx(out=wq[:].bitcast(FP8X4), scales=ws[:], in_=w_bf[:].rearrange("p j m r -> p (j m r)"))
-
-        xq = [keep.tile([P, S // 2], U32, name="xq%d" % u, align_bytes=64) for u in range(2)]
+        xq = keep.tile([P, S], U32, name="xq", tag="w_then_xq", align_bytes=64)
         for u in range(2):
-            nc.vector.tensor_copy(xq[u][:], xw_tab[:].indirect(offs_sb[:, 16 * u : 16 * (u + 1)]))
-        es = keep.tile([P, V], U8, name="es", tag="w_then_es", align_bytes=64)
+            nc.vector.tensor_copy(xq[:, u * HALF : (u + 1) * HALF], xw_tab[:].indirect(offs_sb[:, 16 * u : 16 * (u + 1)]))
+        qa = keep.tile([P, V], F32, name="qa", tag="xw_then_qa", align_bytes=64)
+        nc.vector.tensor_copy(qa[:], qa_tab[:].indirect(refs_sb[:]))
+        eq = keep.tile([P, V], U32, name="eq", tag="qa_then_eq", align_bytes=64)
+        nc.vector.tensor_copy(eq[:], ew_tab[:].indirect(refs_sb[:]))
+        es = keep.tile([P, V], U8, name="es", tag="ew_then_es", align_bytes=64)
         nc.vector.tensor_copy(es[:], es_tab[:].indirect(refs_sb[:]))
 
-        hq = keep.tile([P, S], U32, name="hq", align_bytes=64)
-        hs = keep.tile([P, S], U8, name="hs", align_bytes=64)
-        h_bf = []
+        hq = keep.tile([P, S], U32, name="hq", tag="es_then_hq", align_bytes=64)
+        hs = [keep.tile([P, HALF], U8, name="hs%d" % u, align_bytes=64) for u in range(2)]
+        h_bf = [keep.tile([P, HALF, PACK], BF16, name="h_bf%d" % u, align_bytes=64) for u in range(2)]
         for c in range(NB):
             h_ps = psum.tile([P, PACK, P], F32, name="h_ps%d" % c, tag="h%d" % c)
             cols = slice((c % 2) * P, (c % 2 + 1) * P)
@@ -116,64 +119,75 @@ def tile_picked_ytani_act_p_kernel(
                     out=h_ps[:, j, :],
                     lhsT=wq[:, j * P : (j + 1) * P].bitcast(FP8X4),
                     lhsT_scale=ws[:, j * P : (j + 1) * P],
-                    rhs=xq[c // 2][:, cols].bitcast(FP8X4),
+                    rhs=xq[:, c * P : (c + 1) * P].bitcast(FP8X4),
                     rhs_scale=xs[:, c * P : (c + 1) * P],
                     start=True,
                     stop=True,
                 )
-            hb = keep.tile([P, P, PACK], BF16, name="h_bf%d" % c, align_bytes=64)
-            nc.scalar.copy(out=hb[:], in_=h_ps[:].rearrange("p j n -> p n j"))
-            h_bf.append(hb)
+            nc.scalar.copy(out=h_bf[c // 2][:, cols, :], in_=h_ps[:].rearrange("p j n -> p n j"))
 
-        eq = [keep.tile([P, V // 2], U32, name="eq%d" % u, align_bytes=64) for u in range(2)]
-        for c in range(NB):
-            nc.vector.quantize_mx(
-                out=hq[:, c * P : (c + 1) * P].bitcast(FP8X4),
-                scales=hs[:, c * P : (c + 1) * P],
-                in_=h_bf[c][:].rearrange("p n j -> p (n j)"),
-            )
-            if c % 2 == 0:
-                u = c // 2
-                nc.vector.tensor_copy(eq[u][:], ew_tab[:].indirect(refs_sb[:, 16 * u : 16 * (u + 1)]))
-
-        s_ps, dneg, root, inv, sgn, num, arg = [], [], [], [], [], [], []
+        qa_ps = psum.tile([P, NB, P], F32, name="qa_ps", tag="s1")
         for b in range(NB):
-            sp = psum.tile([P, S], F32, name="s_ps%d" % b, tag="s%d" % b)
-            cols = slice((b % 2) * P, (b % 2 + 1) * P)
-            nc.tensor.matmul_mx(
-                out=sp[:],
-                lhsT=eq[b // 2][:, cols].bitcast(FP8X4),
-                lhsT_scale=es[:, b * P : (b + 1) * P],
-                rhs=hq[:].bitcast(FP8X4),
-                rhs_scale=hs[:],
-                start=True,
-                stop=True,
-            )
+            nc.tensor.transpose(qa_ps[:, b, :], qa[:, b * P : (b + 1) * P], ident[:])
+        qa_col = keep.tile([P, NB, 2], F32, name="qa_col")
+        nc.scalar.activation(qa_col[:], qa_ps[:, :, 0:P:ACT_ROW], ACT.Copy, scale=1.0 / Y_SCALE)
+
+        for u in range(2):
+            nc.vector.quantize_mx(out=hq[:, u * HALF : (u + 1) * HALF].bitcast(FP8X4), scales=hs[u][:], in_=h_bf[u][:].rearrange("p n j -> p (n j)"))
+
+        quads = [(u, g) for u in range(2) for g in range(2)]
+        s_ps, dneg, root, inv, sgn, num, arg = [], [], [], [], [], [], []
+        for n, (u, g) in enumerate(quads):
+            sp = psum.tile([P, 2, HALF], F32, name="s_ps%d" % n, tag="s%d" % n)
+            for e in range(2):
+                b = 2 * g + e
+                nc.tensor.matmul_mx(
+                    out=sp[:, e, :],
+                    lhsT=eq[:, b * P : (b + 1) * P].bitcast(FP8X4),
+                    lhsT_scale=es[:, b * P : (b + 1) * P],
+                    rhs=hq[:, u * HALF : (u + 1) * HALF].bitcast(FP8X4),
+                    rhs_scale=hs[u][:],
+                    start=True,
+                    stop=True,
+                )
             s_ps.append(sp)
             for group, label in ((dneg, "dneg"), (root, "root"), (inv, "inv"), (sgn, "sgn"), (num, "num"), (arg, "arg")):
-                group.append(keep.tile([P, S], F32, name="%s%d" % (label, b), align_bytes=64))
+                group.append(keep.tile([P, 2, HALF], F32, name="%s%d" % (label, n), align_bytes=64))
 
-        for b in range(NB):
-            nc.vector.scalar_tensor_tensor(dneg[b][:], s_ps[b][:], qa_col[:, b, 0:1], own_row[:], ALU.subtract, ALU.subtract)
-            nc.scalar.activation(root[b][:], dneg[b][:], ACT.Abs_reciprocal_sqrt)
-        for b in range(NB):
-            nc.vector.tensor_scalar(sgn[b][:], dneg[b][:], 0.0, 0.5, ALU.is_gt, ALU.subtract)
-            nc.scalar.activation(inv[b][:], root[b][:], ACT.Square)
+        for n, (u, g) in enumerate(quads):
+            for e in range(2):
+                nc.vector.scalar_tensor_tensor(
+                    dneg[n][:, e, :], s_ps[n][:, e, :], qa_col[:, 2 * g + e, 0:1], own_row[:, u * HALF : (u + 1) * HALF], ALU.subtract, ALU.subtract
+                )
+            nc.scalar.activation(root[n][:], dneg[n][:], ACT.Abs_reciprocal_sqrt)
+        for n in range(len(quads)):
+            nc.vector.tensor_scalar(sgn[n][:], dneg[n][:], 0.0, 0.5, ALU.is_gt, ALU.subtract)
+            nc.scalar.activation(inv[n][:], root[n][:], ACT.Square)
 
-        def scale_sums(b):
-            nc.vector.scalar_tensor_tensor(num[b][:], s_ps[b][:], qa_col[:, b, 1:2], inv[b][:], ALU.mult, ALU.mult)
+        def scale_sums(n):
+            g = quads[n][1]
+            for e in range(2):
+                nc.vector.scalar_tensor_tensor(
+                    num[n][:, e, :], s_ps[n][:, e, :], qa_col[:, 2 * g + e, 1:2], inv[n][:, e, :], ALU.mult, ALU.mult
+                )
 
-        def finish(b):
-            nc.vector.tensor_tensor(arg[b][:], num[b][:], sgn[b][:], ALU.mult)
-            o_ps = psum.tile([P, NB, P], F32, name="o_ps%d" % b, tag="h%d" % b)
-            for c in range(NB):
-                nc.tensor.transpose(o_ps[:, c, :], arg[b][:, c * P : (c + 1) * P], ident[:])
-            res = keep.tile([P, NB, P], F32, name="res%d" % b, align_bytes=64)
+        def finish(n, c0, c1, bank):
+            u, g = quads[n]
+            cols = slice(c0 * P, c1 * P)
+            nc.vector.tensor_tensor(arg[n][:, :, cols], num[n][:, :, cols], sgn[n][:, :, cols], ALU.mult)
+            o_ps = psum.tile([P, c1 - c0, HALF], F32, name="o_ps%d_%d" % (n, c0), tag=bank)
+            for c in range(c0, c1):
+                for e in range(2):
+                    nc.tensor.transpose(o_ps[:, c - c0, e * P : (e + 1) * P], arg[n][:, e, c * P : (c + 1) * P], ident[:])
+            res = keep.tile([P, c1 - c0, HALF], F32, name="res%d_%d" % (n, c0), align_bytes=64)
             nc.scalar.activation(res[:], o_ps[:], ACT.Tanh, scale=-2.0 * Y_SCALE)
-            nc.sync.dma_start(out=out[:, b * P : (b + 1) * P].rearrange("(c p) v -> p c v", p=P), in_=res[:])
+            rows = slice(u * HALF + c0 * P, u * HALF + c1 * P)
+            nc.sync.dma_start(out=out[rows, g * HALF : (g + 1) * HALF].rearrange("(c p) v -> p c v", p=P), in_=res[:])
 
+        last = len(quads) - 1
         scale_sums(0)
-        for b in range(1, NB):
-            scale_sums(b)
-            finish(b - 1)
-        finish(NB - 1)
+        for n in range(1, len(quads)):
+            scale_sums(n)
+            finish(n - 1, 0, 2, "h%d" % (n - 1))
+        finish(last, 0, 1, "h%d" % last)
+        finish(last, 1, 2, "s0")

@@ -42,53 +42,49 @@ def tile_picked_ytani_act_p_kernel(
         refs_sb = keep.tile([P, V // 16], U16, name="refs_sb")
         xs_tab = keep.tile([P, T], U8, name="xs_tab", align_bytes=64)
         es_tab = keep.tile([P, W], U8, name="es_tab", tag="es_then_hq", align_bytes=64)
-        qa_tab = keep.tile([P, W], F32, name="qa_tab", tag="qa_then_eq", align_bytes=64)
-        xw_tab = keep.tile([P, T], U32, name="xw_tab", tag="xw_then_qa", align_bytes=64)
-        ew_tab = keep.tile([P, W], U32, name="ew_tab", tag="ew_then_es", align_bytes=64)
-        w_raw = keep.tile([P, PACK, H], F32, name="w_raw", align_bytes=64)
+        qa_tab = keep.tile([P, W], F32, name="qa_tab", tag="qa_then_wq", align_bytes=64)
+        xw_tab = keep.tile([P, T], U32, name="xw_tab", tag="xw_then_es", align_bytes=64)
+        ew_tab = keep.tile([P, W], U32, name="ew_tab", align_bytes=64)
+        w_raw = [keep.tile([P, PACK, HALF], F32, name="w_raw%d" % u, align_bytes=64) for u in range(2)]
         own_col = keep.tile([P, NB], F32, name="own_col")
         ident = keep.tile([P, P], F32, name="ident", align_bytes=64)
         warm_in = keep.tile([P, 1], F32, name="warm_in")
         warm_out = keep.tile([P, 1], F32, name="warm_out")
 
-        nc.gpsimd.memset(xs_tab[:].bitcast(I32), 0)
-        nc.gpsimd.memset(qa_tab[:, : W // 2], 0.0)
-        nc.vector.memset(qa_tab[:, W // 2 :], 0.0)
+        nc.vector.memset(xs_tab[:].bitcast(I32), 0)
         nc.vector.memset(warm_in[:], 1.0)
+        nc.vector.memset(qa_tab[:], 0.0)
         nc.vector.memset(es_tab[:].bitcast(I32), 0)
 
+        w_rows = w1.rearrange("(p r) c -> p r c", r=PACK)
         nc.sync.dma_start(offs_sb[:], offs)
         nc.sync.dma_start(refs_sb[:], refs)
         load_scale_rows((nc.sync, nc.sync, nc.scalar, nc.scalar), xs_tab, x_scales)
-        nc.sync.dma_start(out=w_raw[:], in_=w1.rearrange("(p r) c -> p r c", r=PACK))
-        nc.sync.dma_start(out=xw_tab[:].bitcast(I32), in_=x_words[0].rearrange("p n t -> p (n t)").bitcast(I32))
+        for u in range(2):
+            nc.sync.dma_start(out=w_raw[u][:], in_=w_rows[:, :, u * HALF : (u + 1) * HALF])
         nc.sync.dma_start(out=qa_tab[0:1, :], in_=qn[0:1, :])
         nc.sync.dma_start(out=qa_tab[ACT_ROW : ACT_ROW + 1, :], in_=act[0:1, :])
-        nc.sync.dma_start(out=ew_tab[:].bitcast(I32), in_=e_words[0].rearrange("p n t -> p (n t)").bitcast(I32))
+        nc.sync.dma_start(out=xw_tab[:].bitcast(I32), in_=x_words[0].rearrange("p n t -> p (n t)").bitcast(I32))
         load_scale_rows((nc.sync,) * 4, es_tab, e_scales)
+        nc.sync.dma_start(out=ew_tab[:].bitcast(I32), in_=e_words[0].rearrange("p n t -> p (n t)").bitcast(I32))
         nc.scalar.dma_start(out=own_col[:], in_=own.rearrange("(p c) o -> p (c o)", c=NB))
         nc.scalar.activation(warm_out[:], warm_in[:], ACT.Abs_reciprocal_sqrt)
         make_identity(nc, ident[:])
 
         xs = keep.tile([P, S], U8, name="xs", align_bytes=64)
         nc.vector.tensor_copy(xs[:], xs_tab[:].indirect(offs_sb[:]))
+        qa = keep.tile([P, V], F32, name="qa", align_bytes=64)
+        nc.vector.tensor_copy(qa[:], qa_tab[:].indirect(refs_sb[:]))
 
-        w_view = w_raw[:].rearrange("p r (m j) -> p m j r", j=PACK)
-        w_bf = [
-            keep.tile([P, 2, P, PACK], BF16, name="w_bf0", tag="w_then_xq", align_bytes=64),
-            keep.tile([P, 2, P, PACK], BF16, name="w_bf1", align_bytes=64),
-        ]
-        nc.scalar.copy(out=w_bf[0][:].rearrange("p j m r -> p m j r"), in_=w_view[:, :, 0:2, :])
-        nc.vector.tensor_copy(out=w_bf[1][:].rearrange("p j m r -> p m j r"), in_=w_view[:, :, 2:4, :])
-
-        wq = keep.tile([P, H], U32, name="wq", align_bytes=64)
-        ws = keep.tile([P, H], U8, name="ws", align_bytes=64)
-        for a in (1, 0):
-            nc.vector.quantize_mx(
-                out=wq[:, a * HALF : (a + 1) * HALF].bitcast(FP8X4),
-                scales=ws[:, a * HALF : (a + 1) * HALF],
-                in_=w_bf[a][:].rearrange("p j m r -> p (j m r)"),
+        w_bf = keep.tile([P, PACK, P, PACK], BF16, name="w_bf", tag="w_then_xq", align_bytes=64)
+        for u in range(2):
+            nc.scalar.copy(
+                out=w_bf[:, :, u * (P // 2) : (u + 1) * (P // 2), :].rearrange("p j m r -> p m j r"),
+                in_=w_raw[u][:].rearrange("p r (m j) -> p m j r", j=PACK),
             )
+        wq = keep.tile([P, H], U32, name="wq", tag="qa_then_wq", align_bytes=64)
+        ws = keep.tile([P, H], U8, name="ws", align_bytes=64)
+        nc.vector.quantize_mx(out=wq[:].bitcast(FP8X4), scales=ws[:], in_=w_bf[:].rearrange("p j m r -> p (j m r)"))
 
         own_ps = psum.tile([P, NB, P], F32, name="own_ps", tag="s0")
         for c in range(NB):
@@ -97,16 +93,18 @@ def tile_picked_ytani_act_p_kernel(
         nc.scalar.activation(
             own_row[:].rearrange("p (n c) -> p n c", c=NB), own_ps[:].rearrange("p c n -> p n c"), ACT.Copy, scale=1.0 / Y_SCALE
         )
+        qa_ps = psum.tile([P, NB, P], F32, name="qa_ps", tag="s1")
+        for b in range(NB):
+            nc.tensor.transpose(qa_ps[:, b, :], qa[:, b * P : (b + 1) * P], ident[:])
+        qa_col = keep.tile([P, NB, 2], F32, name="qa_col")
+        nc.scalar.activation(qa_col[:], qa_ps[:, :, 0:P:ACT_ROW], ACT.Copy, scale=1.0 / Y_SCALE)
 
         xq = keep.tile([P, S], U32, name="xq", tag="w_then_xq", align_bytes=64)
         for u in range(2):
             nc.vector.tensor_copy(xq[:, u * HALF : (u + 1) * HALF], xw_tab[:].indirect(offs_sb[:, 16 * u : 16 * (u + 1)]))
-        qa = keep.tile([P, V], F32, name="qa", tag="xw_then_qa", align_bytes=64)
-        nc.vector.tensor_copy(qa[:], qa_tab[:].indirect(refs_sb[:]))
-        eq = keep.tile([P, V], U32, name="eq", tag="qa_then_eq", align_bytes=64)
-        nc.vector.tensor_copy(eq[:], ew_tab[:].indirect(refs_sb[:]))
-        es = keep.tile([P, V], U8, name="es", tag="ew_then_es", align_bytes=64)
+        es = keep.tile([P, V], U8, name="es", tag="xw_then_es", align_bytes=64)
         nc.vector.tensor_copy(es[:], es_tab[:].indirect(refs_sb[:]))
+        eq = keep.tile([P, V], U32, name="eq", align_bytes=64)
 
         hq = keep.tile([P, S], U32, name="hq", tag="es_then_hq", align_bytes=64)
         hs = [keep.tile([P, HALF], U8, name="hs%d" % u, align_bytes=64) for u in range(2)]
@@ -126,13 +124,8 @@ def tile_picked_ytani_act_p_kernel(
                 )
             nc.scalar.copy(out=h_bf[c // 2][:, cols, :], in_=h_ps[:].rearrange("p j n -> p n j"))
 
-        qa_ps = psum.tile([P, NB, P], F32, name="qa_ps", tag="s1")
-        for b in range(NB):
-            nc.tensor.transpose(qa_ps[:, b, :], qa[:, b * P : (b + 1) * P], ident[:])
-        qa_col = keep.tile([P, NB, 2], F32, name="qa_col")
-        nc.scalar.activation(qa_col[:], qa_ps[:, :, 0:P:ACT_ROW], ACT.Copy, scale=1.0 / Y_SCALE)
-
         for u in range(2):
+            nc.vector.tensor_copy(eq[:, u * HALF : (u + 1) * HALF], ew_tab[:].indirect(refs_sb[:, 16 * u : 16 * (u + 1)]))
             nc.vector.quantize_mx(out=hq[:, u * HALF : (u + 1) * HALF].bitcast(FP8X4), scales=hs[u][:], in_=h_bf[u][:].rearrange("p n j -> p (n j)"))
 
         quads = [(u, g) for u in range(2) for g in range(2)]
@@ -160,9 +153,15 @@ def tile_picked_ytani_act_p_kernel(
                     dneg[n][:, e, :], s_ps[n][:, e, :], qa_col[:, 2 * g + e, 0:1], own_row[:, u * HALF : (u + 1) * HALF], ALU.subtract, ALU.subtract
                 )
             nc.scalar.activation(root[n][:], dneg[n][:], ACT.Abs_reciprocal_sqrt)
-        for n in range(len(quads)):
+        last = len(quads) - 1
+
+        def half_sign(n):
             nc.vector.tensor_scalar(sgn[n][:], dneg[n][:], 0.0, 0.5, ALU.is_gt, ALU.subtract)
+
+        for n in range(len(quads)):
             nc.scalar.activation(inv[n][:], root[n][:], ACT.Square)
+        for n in range(last):
+            half_sign(n)
 
         def scale_sums(n):
             g = quads[n][1]
@@ -184,10 +183,12 @@ def tile_picked_ytani_act_p_kernel(
             rows = slice(u * HALF + c0 * P, u * HALF + c1 * P)
             nc.sync.dma_start(out=out[rows, g * HALF : (g + 1) * HALF].rearrange("(c p) v -> p c v", p=P), in_=res[:])
 
-        last = len(quads) - 1
         scale_sums(0)
-        for n in range(1, len(quads)):
+        for n in range(1, last):
             scale_sums(n)
             finish(n - 1, 0, 2, "h%d" % (n - 1))
+        finish(last - 1, 0, 2, "h%d" % (last - 1))
+        scale_sums(last)
+        half_sign(last)
         finish(last, 0, 1, "h%d" % last)
         finish(last, 1, 2, "s0")

@@ -44,7 +44,7 @@ def tile_picked_ytani_act_p_kernel(
         es_tab = keep.tile([P, W], U8, name="es_tab", tag="es_then_hq", align_bytes=64)
         qa_tab = keep.tile([P, W], F32, name="qa_tab", tag="qa_then_wq", align_bytes=64)
         xw_tab = keep.tile([P, T], U32, name="xw_tab", tag="xw_then_es", align_bytes=64)
-        ew_tab = keep.tile([P, W], U32, name="ew_tab", align_bytes=64)
+        ew_tab = keep.tile([P, W], U32, name="ew_tab", tag="ew_then_hq", align_bytes=64)
         w_raw = [keep.tile([P, PACK, HALF], F32, name="w_raw%d" % u, align_bytes=64) for u in range(2)]
         own_col = keep.tile([P, NB], F32, name="own_col")
         ident = keep.tile([P, P], F32, name="ident", align_bytes=64)
@@ -77,11 +77,17 @@ def tile_picked_ytani_act_p_kernel(
         nc.vector.tensor_copy(qa[:], qa_tab[:].indirect(refs_sb[:]))
 
         w_bf = keep.tile([P, PACK, P, PACK], BF16, name="w_bf", tag="w_then_xq", align_bytes=64)
-        for u in range(2):
-            nc.scalar.copy(
-                out=w_bf[:, :, u * (P // 2) : (u + 1) * (P // 2), :].rearrange("p j m r -> p m j r"),
-                in_=w_raw[u][:].rearrange("p r (m j) -> p m j r", j=PACK),
+
+        def cast_w(copy, m0, m1):
+            u, base = divmod(m0, P // 2)
+            copy(
+                out=w_bf[:, :, m0:m1, :].rearrange("p j m r -> p m j r"),
+                in_=w_raw[u][:, :, PACK * base : PACK * (base + m1 - m0)].rearrange("p r (m j) -> p m j r", j=PACK),
             )
+
+        cast_w(nc.scalar.copy, 0, 64)
+        cast_w(nc.scalar.copy, 64, 96)
+        cast_w(nc.vector.tensor_copy, 96, 128)
         wq = keep.tile([P, H], U32, name="wq", tag="qa_then_wq", align_bytes=64)
         ws = keep.tile([P, H], U8, name="ws", align_bytes=64)
         nc.vector.quantize_mx(out=wq[:].bitcast(FP8X4), scales=ws[:], in_=w_bf[:].rearrange("p j m r -> p (j m r)"))
@@ -106,7 +112,10 @@ def tile_picked_ytani_act_p_kernel(
         nc.vector.tensor_copy(es[:], es_tab[:].indirect(refs_sb[:]))
         eq = keep.tile([P, V], U32, name="eq", align_bytes=64)
 
-        hq = keep.tile([P, S], U32, name="hq", tag="es_then_hq", align_bytes=64)
+        hq = [
+            keep.tile([P, HALF], U32, name="hq0", tag="es_then_hq", align_bytes=64),
+            keep.tile([P, HALF], U32, name="hq1", tag="ew_then_hq", align_bytes=64),
+        ]
         hs = [keep.tile([P, HALF], U8, name="hs%d" % u, align_bytes=64) for u in range(2)]
         h_bf = [keep.tile([P, HALF, PACK], BF16, name="h_bf%d" % u, align_bytes=64) for u in range(2)]
         for c in range(NB):
@@ -124,9 +133,13 @@ def tile_picked_ytani_act_p_kernel(
                 )
             nc.scalar.copy(out=h_bf[c // 2][:, cols, :], in_=h_ps[:].rearrange("p j n -> p n j"))
 
-        for u in range(2):
-            nc.vector.tensor_copy(eq[:, u * HALF : (u + 1) * HALF], ew_tab[:].indirect(refs_sb[:, 16 * u : 16 * (u + 1)]))
-            nc.vector.quantize_mx(out=hq[:, u * HALF : (u + 1) * HALF].bitcast(FP8X4), scales=hs[u][:], in_=h_bf[u][:].rearrange("p n j -> p (n j)"))
+        def quantize_h(u):
+            nc.vector.quantize_mx(out=hq[u][:].bitcast(FP8X4), scales=hs[u][:], in_=h_bf[u][:].rearrange("p n j -> p (n j)"))
+
+        quantize_h(0)
+        for g in range(2):
+            nc.vector.tensor_copy(eq[:, g * HALF : (g + 1) * HALF], ew_tab[:].indirect(refs_sb[:, 16 * g : 16 * (g + 1)]))
+        quantize_h(1)
 
         quads = [(u, g) for u in range(2) for g in range(2)]
         s_ps, dneg, root, inv, sgn, num, arg = [], [], [], [], [], [], []
@@ -138,7 +151,7 @@ def tile_picked_ytani_act_p_kernel(
                     out=sp[:, e, :],
                     lhsT=eq[:, b * P : (b + 1) * P].bitcast(FP8X4),
                     lhsT_scale=es[:, b * P : (b + 1) * P],
-                    rhs=hq[:, u * HALF : (u + 1) * HALF].bitcast(FP8X4),
+                    rhs=hq[u][:].bitcast(FP8X4),
                     rhs_scale=hs[u][:],
                     start=True,
                     stop=True,

@@ -22,12 +22,14 @@ PACK = 4
 NB = 4
 HALF = 256
 Y_SCALE = 0.3
-ACT_ROW = 64
+QN_ROW = 8
+ACT_ROW = 76
+E_PLANE = 4
 
 
-def load_scale_rows(queues, plane, rows):
-    for q, queue in enumerate(queues):
-        queue.dma_start(out=plane[32 * q : 32 * q + 4, :].bitcast(I32), in_=rows[0, 4 * q : 4 * q + 4, :].bitcast(I32))
+def load_scale_rows(queues, plane, first, rows):
+    for r, queue in enumerate(queues):
+        queue.dma_start(out=plane[first + r : P : 32, :].bitcast(I32), in_=rows[0, r:16:4, :].bitcast(I32))
 
 
 def tile_picked_ytani_act_p_kernel(
@@ -44,7 +46,7 @@ def tile_picked_ytani_act_p_kernel(
         es_tab = keep.tile([P, W], U8, name="es_tab", tag="es_then_hq", align_bytes=64)
         qa_tab = keep.tile([P, W], F32, name="qa_tab", tag="qa_then_wq", align_bytes=64)
         xw_tab = keep.tile([P, T], U32, name="xw_tab", tag="xw_then_es", align_bytes=64)
-        ew_tab = keep.tile([P, W], U32, name="ew_tab", tag="ew_then_hq", align_bytes=64)
+        ew_tab = keep.tile([P, W], U32, name="ew_tab", align_bytes=64)
         w_raw = [keep.tile([P, PACK, HALF], F32, name="w_raw%d" % u, align_bytes=64) for u in range(2)]
         own_col = keep.tile([P, NB], F32, name="own_col")
         ident = keep.tile([P, P], F32, name="ident", align_bytes=64)
@@ -59,15 +61,15 @@ def tile_picked_ytani_act_p_kernel(
         w_rows = w1.rearrange("(p r) c -> p r c", r=PACK)
         nc.sync.dma_start(offs_sb[:], offs)
         nc.sync.dma_start(refs_sb[:], refs)
-        load_scale_rows((nc.sync, nc.sync, nc.scalar, nc.scalar), xs_tab, x_scales)
+        load_scale_rows((nc.sync, nc.sync, nc.scalar, nc.scalar), xs_tab, 0, x_scales)
         for u in range(2):
             nc.sync.dma_start(out=w_raw[u][:], in_=w_rows[:, :, u * HALF : (u + 1) * HALF])
-        nc.sync.dma_start(out=qa_tab[0:1, :], in_=qn[0:1, :])
+        nc.sync.dma_start(out=own_col[:], in_=own.rearrange("(p c) o -> p (c o)", c=NB))
+        nc.sync.dma_start(out=qa_tab[QN_ROW : QN_ROW + 1, :], in_=qn[0:1, :])
         nc.sync.dma_start(out=qa_tab[ACT_ROW : ACT_ROW + 1, :], in_=act[0:1, :])
         nc.sync.dma_start(out=xw_tab[:].bitcast(I32), in_=x_words[0].rearrange("p n t -> p (n t)").bitcast(I32))
-        load_scale_rows((nc.sync,) * 4, es_tab, e_scales)
+        load_scale_rows((nc.sync,) * 4, es_tab, E_PLANE, e_scales)
         nc.sync.dma_start(out=ew_tab[:].bitcast(I32), in_=e_words[0].rearrange("p n t -> p (n t)").bitcast(I32))
-        nc.scalar.dma_start(out=own_col[:], in_=own.rearrange("(p c) o -> p (c o)", c=NB))
         nc.scalar.activation(warm_out[:], warm_in[:], ACT.Abs_reciprocal_sqrt)
         make_identity(nc, ident[:])
 
@@ -86,8 +88,7 @@ def tile_picked_ytani_act_p_kernel(
             )
 
         cast_w(nc.scalar.copy, 0, 64)
-        cast_w(nc.scalar.copy, 64, 96)
-        cast_w(nc.vector.tensor_copy, 96, 128)
+        cast_w(nc.scalar.copy, 64, 128)
         wq = keep.tile([P, H], U32, name="wq", tag="qa_then_wq", align_bytes=64)
         ws = keep.tile([P, H], U8, name="ws", align_bytes=64)
         nc.vector.quantize_mx(out=wq[:].bitcast(FP8X4), scales=ws[:], in_=w_bf[:].rearrange("p j m r -> p (j m r)"))
@@ -95,26 +96,35 @@ def tile_picked_ytani_act_p_kernel(
         own_ps = psum.tile([P, NB, P], F32, name="own_ps", tag="s0")
         for c in range(NB):
             nc.tensor.transpose(own_ps[:, c, :], own_col[:, c : c + 1].to_broadcast([P, P]), ident[:])
-        own_row = keep.tile([P, S], F32, name="own_row", align_bytes=64)
-        nc.scalar.activation(
-            own_row[:].rearrange("p (n c) -> p n c", c=NB), own_ps[:].rearrange("p c n -> p n c"), ACT.Copy, scale=1.0 / Y_SCALE
-        )
+        own_row = [
+            keep.tile([P, HALF], F32, name="own_row0", tag="own_then_hq", align_bytes=64),
+            keep.tile([P, HALF], F32, name="own_row1", align_bytes=64),
+        ]
+        for u in range(2):
+            nc.scalar.activation(
+                own_row[u][:].rearrange("p (n c) -> p n c", c=NB),
+                own_ps[:, :, u * 64 : (u + 1) * 64].rearrange("p c n -> p n c"),
+                ACT.Copy,
+                scale=1.0 / Y_SCALE,
+            )
         qa_ps = psum.tile([P, NB, P], F32, name="qa_ps", tag="s1")
         for b in range(NB):
             nc.tensor.transpose(qa_ps[:, b, :], qa[:, b * P : (b + 1) * P], ident[:])
         qa_col = keep.tile([P, NB, 2], F32, name="qa_col")
-        nc.scalar.activation(qa_col[:], qa_ps[:, :, 0:P:ACT_ROW], ACT.Copy, scale=1.0 / Y_SCALE)
+        nc.scalar.activation(qa_col[:], qa_ps[:, :, QN_ROW : ACT_ROW + 1 : ACT_ROW - QN_ROW], ACT.Copy, scale=1.0 / Y_SCALE)
 
-        xq = keep.tile([P, S], U32, name="xq", tag="w_then_xq", align_bytes=64)
+        xq = [
+            keep.tile([P, HALF], U32, name="xq0", tag="w_then_xq", align_bytes=64),
+            keep.tile([P, HALF], U32, name="xq1", align_bytes=64),
+        ]
         for u in range(2):
-            nc.vector.tensor_copy(xq[:, u * HALF : (u + 1) * HALF], xw_tab[:].indirect(offs_sb[:, 16 * u : 16 * (u + 1)]))
+            nc.vector.tensor_copy(xq[u][:], xw_tab[:].indirect(offs_sb[:, 16 * u : 16 * (u + 1)]))
         es = keep.tile([P, V], U8, name="es", tag="xw_then_es", align_bytes=64)
         nc.vector.tensor_copy(es[:], es_tab[:].indirect(refs_sb[:]))
-        eq = keep.tile([P, V], U32, name="eq", align_bytes=64)
+        eq = [keep.tile([P, HALF], U32, name="eq%d" % g, align_bytes=64) for g in range(2)]
 
         hq = [
             keep.tile([P, HALF], U32, name="hq0", tag="es_then_hq", align_bytes=64),
-            keep.tile([P, HALF], U32, name="hq1", tag="ew_then_hq", align_bytes=64),
         ]
         hs = [keep.tile([P, HALF], U8, name="hs%d" % u, align_bytes=64) for u in range(2)]
         h_bf = [keep.tile([P, HALF, PACK], BF16, name="h_bf%d" % u, align_bytes=64) for u in range(2)]
@@ -126,7 +136,7 @@ def tile_picked_ytani_act_p_kernel(
                     out=h_ps[:, j, :],
                     lhsT=wq[:, j * P : (j + 1) * P].bitcast(FP8X4),
                     lhsT_scale=ws[:, j * P : (j + 1) * P],
-                    rhs=xq[:, c * P : (c + 1) * P].bitcast(FP8X4),
+                    rhs=xq[c // 2][:, cols].bitcast(FP8X4),
                     rhs_scale=xs[:, c * P : (c + 1) * P],
                     start=True,
                     stop=True,
@@ -138,43 +148,45 @@ def tile_picked_ytani_act_p_kernel(
 
         quantize_h(0)
         for g in range(2):
-            nc.vector.tensor_copy(eq[:, g * HALF : (g + 1) * HALF], ew_tab[:].indirect(refs_sb[:, 16 * g : 16 * (g + 1)]))
-        quantize_h(1)
+            nc.vector.tensor_copy(eq[g][:], ew_tab[:].indirect(refs_sb[:, 16 * g : 16 * (g + 1)]))
 
         quads = [(u, g) for u in range(2) for g in range(2)]
         s_ps, dneg, root, inv, sgn, num, arg = [], [], [], [], [], [], []
-        for n, (u, g) in enumerate(quads):
+        for n in range(len(quads)):
+            for group, label in ((dneg, "dneg"), (root, "root"), (inv, "inv"), (sgn, "sgn"), (num, "num"), (arg, "arg")):
+                group.append(keep.tile([P, 2, HALF], F32, name="%s%d" % (label, n), align_bytes=64))
+
+        def product(n):
+            u, g = quads[n]
             sp = psum.tile([P, 2, HALF], F32, name="s_ps%d" % n, tag="s%d" % n)
             for e in range(2):
                 b = 2 * g + e
                 nc.tensor.matmul_mx(
                     out=sp[:, e, :],
-                    lhsT=eq[:, b * P : (b + 1) * P].bitcast(FP8X4),
-                    lhsT_scale=es[:, b * P : (b + 1) * P],
+                    lhsT=eq[g][:, e * P : (e + 1) * P].bitcast(FP8X4),
+                    lhsT_scale=es[E_PLANE:P, b * P : (b + 1) * P],
                     rhs=hq[u][:].bitcast(FP8X4),
                     rhs_scale=hs[u][:],
                     start=True,
                     stop=True,
                 )
             s_ps.append(sp)
-            for group, label in ((dneg, "dneg"), (root, "root"), (inv, "inv"), (sgn, "sgn"), (num, "num"), (arg, "arg")):
-                group.append(keep.tile([P, 2, HALF], F32, name="%s%d" % (label, n), align_bytes=64))
 
-        for n, (u, g) in enumerate(quads):
+        def denominators(n):
+            u, g = quads[n]
             for e in range(2):
                 nc.vector.scalar_tensor_tensor(
-                    dneg[n][:, e, :], s_ps[n][:, e, :], qa_col[:, 2 * g + e, 0:1], own_row[:, u * HALF : (u + 1) * HALF], ALU.subtract, ALU.subtract
+                    dneg[n][:, e, :], s_ps[n][:, e, :], qa_col[:, 2 * g + e, 0:1], own_row[u][:], ALU.subtract, ALU.subtract
                 )
+
+        def roots(n):
             nc.scalar.activation(root[n][:], dneg[n][:], ACT.Abs_reciprocal_sqrt)
-        last = len(quads) - 1
+
+        def squares(n):
+            nc.scalar.activation(inv[n][:], root[n][:], ACT.Square)
 
         def half_sign(n):
             nc.vector.tensor_scalar(sgn[n][:], dneg[n][:], 0.0, 0.5, ALU.is_gt, ALU.subtract)
-
-        for n in range(len(quads)):
-            nc.scalar.activation(inv[n][:], root[n][:], ACT.Square)
-        for n in range(last):
-            half_sign(n)
 
         def scale_sums(n):
             g = quads[n][1]
@@ -196,12 +208,34 @@ def tile_picked_ytani_act_p_kernel(
             rows = slice(u * HALF + c0 * P, u * HALF + c1 * P)
             nc.sync.dma_start(out=out[rows, g * HALF : (g + 1) * HALF].rearrange("(c p) v -> p c v", p=P), in_=res[:])
 
+        product(0)
+        product(1)
+        denominators(0)
+        denominators(1)
+        hq.append(keep.tile([P, HALF], U32, name="hq1", tag="own_then_hq", align_bytes=64))
+        quantize_h(1)
+        product(2)
+        product(3)
+        roots(0)
+        roots(1)
+        squares(0)
+        squares(1)
+        half_sign(0)
+        half_sign(1)
+        denominators(2)
+        denominators(3)
+        roots(2)
+        roots(3)
+        squares(2)
+        squares(3)
         scale_sums(0)
-        for n in range(1, last):
-            scale_sums(n)
-            finish(n - 1, 0, 2, "h%d" % (n - 1))
-        finish(last - 1, 0, 2, "h%d" % (last - 1))
-        scale_sums(last)
-        half_sign(last)
-        finish(last, 0, 1, "h%d" % last)
-        finish(last, 1, 2, "s0")
+        scale_sums(1)
+        finish(0, 0, 2, "h0")
+        half_sign(2)
+        finish(1, 0, 2, "h1")
+        scale_sums(2)
+        half_sign(3)
+        scale_sums(3)
+        finish(2, 0, 2, "h2")
+        finish(3, 0, 1, "h3")
+        finish(3, 1, 2, "s0")

@@ -22,14 +22,16 @@ PACK = 4
 NB = 4
 HALF = 256
 Y_SCALE = 0.3
-QN_ROW = 8
-ACT_ROW = 76
-E_PLANE = 4
+QN_ROW = 0
+ACT_ROW = 64
+E_PLANE = 0
 
 
 def load_scale_rows(queues, plane, first, rows):
-    for r, queue in enumerate(queues):
-        queue.dma_start(out=plane[first + r : P : 32, :].bitcast(I32), in_=rows[0, r:16:4, :].bitcast(I32))
+    for q, queue in enumerate(queues):
+        queue.dma_start(
+            out=plane[32 * q + first : 32 * q + first + 4, :].bitcast(I32), in_=rows[0, 4 * q : 4 * q + 4, :].bitcast(I32)
+        )
 
 
 def tile_picked_ytani_act_p_kernel(
@@ -38,38 +40,46 @@ def tile_picked_ytani_act_p_kernel(
     nc = tc.nc
     with ExitStack() as ctx:
         keep = ctx.enter_context(tc.tile_pool(name="keep", bufs=1))
+        late = ctx.enter_context(tc.tile_pool(name="late", bufs=1))
         psum = ctx.enter_context(tc.psum_pool(name="psum", bufs=1))
 
         offs_sb = keep.tile([P, S // 16], U16, name="offs_sb")
         refs_sb = keep.tile([P, V // 16], U16, name="refs_sb")
         xs_tab = keep.tile([P, T], U8, name="xs_tab", align_bytes=64)
-        es_tab = keep.tile([P, W], U8, name="es_tab", tag="es_then_hq", align_bytes=64)
-        qa_tab = keep.tile([P, W], F32, name="qa_tab", tag="qa_then_wq", align_bytes=64)
+        es_tab = keep.tile([P, W], U8, name="es_tab", align_bytes=64)
+        qa_tab = keep.tile([P, W], F32, name="qa_tab", align_bytes=64)
         xw_tab = keep.tile([P, T], U32, name="xw_tab", tag="xw_then_es", align_bytes=64)
         ew_tab = keep.tile([P, W], U32, name="ew_tab", align_bytes=64)
         w_raw = [keep.tile([P, PACK, HALF], F32, name="w_raw%d" % u, align_bytes=64) for u in range(2)]
-        own_col = keep.tile([P, NB], F32, name="own_col")
+        own_col = [keep.tile([P, 2], F32, name="own_col%d" % u) for u in range(2)]
+        own_late = late.tile([P, HALF + 32], F32, name="own_late", offset=4 * HALF - 64, align_bytes=64)
+        own_halves = own.rearrange("(u p c) o -> u p (c o)", u=2, c=2)
         ident = keep.tile([P, P], F32, name="ident", align_bytes=64)
         warm_in = keep.tile([P, 1], F32, name="warm_in")
         warm_out = keep.tile([P, 1], F32, name="warm_out")
 
         nc.vector.memset(xs_tab[:].bitcast(I32), 0)
         nc.vector.memset(warm_in[:], 1.0)
-        nc.vector.memset(qa_tab[:], 0.0)
+        zeros = keep.tile([P, HALF], F32, name="zeros", align_bytes=64)
+        nc.gpsimd.memset(zeros[:], 0.0)
+        nc.vector.tensor_copy(
+            qa_tab[:].rearrange("p (a b) -> p a b", b=HALF), zeros[:].unsqueeze(1).to_broadcast([P, W // HALF, HALF])
+        )
         nc.vector.memset(es_tab[:].bitcast(I32), 0)
 
         w_rows = w1.rearrange("(p r) c -> p r c", r=PACK)
         nc.sync.dma_start(offs_sb[:], offs)
         nc.sync.dma_start(refs_sb[:], refs)
         load_scale_rows((nc.sync, nc.sync, nc.scalar, nc.scalar), xs_tab, 0, x_scales)
-        for u in range(2):
-            nc.sync.dma_start(out=w_raw[u][:], in_=w_rows[:, :, u * HALF : (u + 1) * HALF])
-        nc.sync.dma_start(out=own_col[:], in_=own.rearrange("(p c) o -> p (c o)", c=NB))
+        nc.sync.dma_start(out=w_raw[0][:], in_=w_rows[:, :, 0:HALF])
         nc.sync.dma_start(out=qa_tab[QN_ROW : QN_ROW + 1, :], in_=qn[0:1, :])
         nc.sync.dma_start(out=qa_tab[ACT_ROW : ACT_ROW + 1, :], in_=act[0:1, :])
+        nc.sync.dma_start(out=w_raw[1][:], in_=w_rows[:, :, HALF : 2 * HALF])
+        nc.sync.dma_start(out=own_col[0][:], in_=own_halves[0])
         nc.sync.dma_start(out=xw_tab[:].bitcast(I32), in_=x_words[0].rearrange("p n t -> p (n t)").bitcast(I32))
         load_scale_rows((nc.sync,) * 4, es_tab, E_PLANE, e_scales)
         nc.sync.dma_start(out=ew_tab[:].bitcast(I32), in_=e_words[0].rearrange("p n t -> p (n t)").bitcast(I32))
+        nc.sync.dma_start(out=own_late[:, 0:2], in_=own_halves[1])
         nc.scalar.activation(warm_out[:], warm_in[:], ACT.Abs_reciprocal_sqrt)
         make_identity(nc, ident[:])
 
@@ -78,7 +88,7 @@ def tile_picked_ytani_act_p_kernel(
         qa = keep.tile([P, V], F32, name="qa", align_bytes=64)
         nc.vector.tensor_copy(qa[:], qa_tab[:].indirect(refs_sb[:]))
 
-        w_bf = keep.tile([P, PACK, P, PACK], BF16, name="w_bf", tag="w_then_xq", align_bytes=64)
+        w_bf = keep.tile([P, PACK, P, PACK], BF16, name="w_bf", align_bytes=64)
 
         def cast_w(copy, m0, m1):
             u, base = divmod(m0, P // 2)
@@ -88,44 +98,38 @@ def tile_picked_ytani_act_p_kernel(
             )
 
         cast_w(nc.scalar.copy, 0, 64)
-        cast_w(nc.scalar.copy, 64, 128)
-        wq = keep.tile([P, H], U32, name="wq", tag="qa_then_wq", align_bytes=64)
+        cast_w(nc.scalar.copy, 64, 96)
+        cast_w(nc.vector.tensor_copy, 96, 128)
+        wq = keep.tile([P, H], U32, name="wq", align_bytes=64)
         ws = keep.tile([P, H], U8, name="ws", align_bytes=64)
         nc.vector.quantize_mx(out=wq[:].bitcast(FP8X4), scales=ws[:], in_=w_bf[:].rearrange("p j m r -> p (j m r)"))
 
-        own_ps = psum.tile([P, NB, P], F32, name="own_ps", tag="s0")
-        for c in range(NB):
-            nc.tensor.transpose(own_ps[:, c, :], own_col[:, c : c + 1].to_broadcast([P, P]), ident[:])
-        own_row = [
-            keep.tile([P, HALF], F32, name="own_row0", tag="own_then_hq", align_bytes=64),
-            keep.tile([P, HALF], F32, name="own_row1", align_bytes=64),
-        ]
-        for u in range(2):
+        own_row = [keep.tile([P, HALF], F32, name="own_row%d" % u, align_bytes=64) for u in range(2)]
+
+        def spread_own(u, bank, scale):
+            own_ps = psum.tile([P, 2, P], F32, name="own_ps%d" % u, tag=bank)
+            for c in range(2):
+                nc.tensor.transpose(own_ps[:, c, :], own_col[u][:, c : c + 1].to_broadcast([P, P]), ident[:])
             nc.scalar.activation(
-                own_row[u][:].rearrange("p (n c) -> p n c", c=NB),
-                own_ps[:, :, u * 64 : (u + 1) * 64].rearrange("p c n -> p n c"),
-                ACT.Copy,
-                scale=1.0 / Y_SCALE,
+                own_row[u][:].rearrange("p (n c) -> p n c", c=2), own_ps[:].rearrange("p c n -> p n c"), ACT.Copy, scale=scale
             )
-        qa_ps = psum.tile([P, NB, P], F32, name="qa_ps", tag="s1")
+
+        spread_own(0, "s0", 1.0 / Y_SCALE)
+        qa_ps = psum.tile([P, NB, P], F32, name="qa_ps", tag="s0")
         for b in range(NB):
             nc.tensor.transpose(qa_ps[:, b, :], qa[:, b * P : (b + 1) * P], ident[:])
         qa_col = keep.tile([P, NB, 2], F32, name="qa_col")
         nc.scalar.activation(qa_col[:], qa_ps[:, :, QN_ROW : ACT_ROW + 1 : ACT_ROW - QN_ROW], ACT.Copy, scale=1.0 / Y_SCALE)
 
         xq = [
-            keep.tile([P, HALF], U32, name="xq0", tag="w_then_xq", align_bytes=64),
+            keep.tile([P, HALF], U32, name="xq0", align_bytes=64),
             keep.tile([P, HALF], U32, name="xq1", align_bytes=64),
         ]
         for u in range(2):
             nc.vector.tensor_copy(xq[u][:], xw_tab[:].indirect(offs_sb[:, 16 * u : 16 * (u + 1)]))
         es = keep.tile([P, V], U8, name="es", tag="xw_then_es", align_bytes=64)
         nc.vector.tensor_copy(es[:], es_tab[:].indirect(refs_sb[:]))
-        eq = [keep.tile([P, HALF], U32, name="eq%d" % g, align_bytes=64) for g in range(2)]
 
-        hq = [
-            keep.tile([P, HALF], U32, name="hq0", tag="es_then_hq", align_bytes=64),
-        ]
         hs = [keep.tile([P, HALF], U8, name="hs%d" % u, align_bytes=64) for u in range(2)]
         h_bf = [keep.tile([P, HALF, PACK], BF16, name="h_bf%d" % u, align_bytes=64) for u in range(2)]
         for c in range(NB):
@@ -146,9 +150,21 @@ def tile_picked_ytani_act_p_kernel(
         def quantize_h(u):
             nc.vector.quantize_mx(out=hq[u][:].bitcast(FP8X4), scales=hs[u][:], in_=h_bf[u][:].rearrange("p n j -> p (n j)"))
 
-        quantize_h(0)
-        for g in range(2):
+        def gather_e(g):
             nc.vector.tensor_copy(eq[g][:], ew_tab[:].indirect(refs_sb[:, 16 * g : 16 * (g + 1)]))
+
+        eq = [keep.tile([P, HALF], U32, name="eq0", align_bytes=64)]
+        gather_e(0)
+        nc.vector.tensor_scalar_mul(own_col[1][:], own_late[:, 0:2], 1.0 / Y_SCALE)
+        hq = [
+            late.tile([P, HALF], U32, name="hq0", offset=0, align_bytes=64),
+            late.tile([P, HALF], U32, name="hq1", offset=8 * HALF, align_bytes=64),
+        ]
+        eq.append(late.tile([P, HALF], U32, name="eq1", offset=4 * HALF, align_bytes=64))
+        quantize_h(0)
+        gather_e(1)
+        quantize_h(1)
+        spread_own(1, "s3", 1.0)
 
         quads = [(u, g) for u in range(2) for g in range(2)]
         s_ps, dneg, root, inv, sgn, num, arg = [], [], [], [], [], [], []
@@ -158,11 +174,15 @@ def tile_picked_ytani_act_p_kernel(
 
         def product(n):
             u, g = quads[n]
-            sp = psum.tile([P, 2, HALF], F32, name="s_ps%d" % n, tag="s%d" % n)
+            if n == 0:
+                sp = [psum.tile([P, HALF], F32, name="s_ps0_%d" % e, tag=bank)[:] for e, bank in enumerate(("h0", "s0"))]
+            else:
+                both = psum.tile([P, 2, HALF], F32, name="s_ps%d" % n, tag="s%d" % n)
+                sp = [both[:, e, :] for e in range(2)]
             for e in range(2):
                 b = 2 * g + e
                 nc.tensor.matmul_mx(
-                    out=sp[:, e, :],
+                    out=sp[e],
                     lhsT=eq[g][:, e * P : (e + 1) * P].bitcast(FP8X4),
                     lhsT_scale=es[E_PLANE:P, b * P : (b + 1) * P],
                     rhs=hq[u][:].bitcast(FP8X4),
@@ -176,7 +196,7 @@ def tile_picked_ytani_act_p_kernel(
             u, g = quads[n]
             for e in range(2):
                 nc.vector.scalar_tensor_tensor(
-                    dneg[n][:, e, :], s_ps[n][:, e, :], qa_col[:, 2 * g + e, 0:1], own_row[u][:], ALU.subtract, ALU.subtract
+                    dneg[n][:, e, :], s_ps[n][e], qa_col[:, 2 * g + e, 0:1], own_row[u][:], ALU.subtract, ALU.subtract
                 )
 
         def roots(n):
@@ -188,17 +208,18 @@ def tile_picked_ytani_act_p_kernel(
         def half_sign(n):
             nc.vector.tensor_scalar(sgn[n][:], dneg[n][:], 0.0, 0.5, ALU.is_gt, ALU.subtract)
 
-        def scale_sums(n):
+        def scale_sums(n, e):
             g = quads[n][1]
-            for e in range(2):
-                nc.vector.scalar_tensor_tensor(
-                    num[n][:, e, :], s_ps[n][:, e, :], qa_col[:, 2 * g + e, 1:2], inv[n][:, e, :], ALU.mult, ALU.mult
-                )
+            nc.vector.scalar_tensor_tensor(
+                num[n][:, e, :], s_ps[n][e], qa_col[:, 2 * g + e, 1:2], inv[n][:, e, :], ALU.mult, ALU.mult
+            )
+
+        def apply_sign(n, e0, e1, c0=0, c1=2):
+            cols = slice(c0 * P, c1 * P)
+            nc.vector.tensor_tensor(arg[n][:, e0:e1, cols], num[n][:, e0:e1, cols], sgn[n][:, e0:e1, cols], ALU.mult)
 
         def finish(n, c0, c1, bank):
             u, g = quads[n]
-            cols = slice(c0 * P, c1 * P)
-            nc.vector.tensor_tensor(arg[n][:, :, cols], num[n][:, :, cols], sgn[n][:, :, cols], ALU.mult)
             o_ps = psum.tile([P, c1 - c0, HALF], F32, name="o_ps%d_%d" % (n, c0), tag=bank)
             for c in range(c0, c1):
                 for e in range(2):
@@ -208,34 +229,38 @@ def tile_picked_ytani_act_p_kernel(
             rows = slice(u * HALF + c0 * P, u * HALF + c1 * P)
             nc.sync.dma_start(out=out[rows, g * HALF : (g + 1) * HALF].rearrange("(c p) v -> p c v", p=P), in_=res[:])
 
-        product(0)
-        product(1)
-        denominators(0)
-        denominators(1)
-        hq.append(keep.tile([P, HALF], U32, name="hq1", tag="own_then_hq", align_bytes=64))
-        quantize_h(1)
-        product(2)
-        product(3)
+        for n in range(4):
+            product(n)
+        for n in range(4):
+            denominators(n)
         roots(0)
         roots(1)
         squares(0)
-        squares(1)
-        half_sign(0)
-        half_sign(1)
-        denominators(2)
-        denominators(3)
         roots(2)
+        squares(1)
         roots(3)
         squares(2)
         squares(3)
-        scale_sums(0)
-        scale_sums(1)
-        finish(0, 0, 2, "h0")
+        half_sign(0)
+        half_sign(1)
+        scale_sums(0, 0)
+        scale_sums(0, 1)
         half_sign(2)
-        finish(1, 0, 2, "h1")
-        scale_sums(2)
+        apply_sign(0, 0, 2)
+        finish(0, 0, 2, "h1")
+        scale_sums(1, 0)
+        scale_sums(1, 1)
         half_sign(3)
-        scale_sums(3)
-        finish(2, 0, 2, "h2")
-        finish(3, 0, 1, "h3")
+        apply_sign(1, 0, 2)
+        finish(1, 0, 2, "h2")
+        scale_sums(2, 0)
+        scale_sums(2, 1)
+        scale_sums(3, 0)
+        apply_sign(2, 0, 2)
+        finish(2, 0, 2, "h3")
+        scale_sums(3, 1)
+        apply_sign(3, 0, 1)
+        apply_sign(3, 1, 2, 0, 1)
+        apply_sign(3, 1, 2, 1, 2)
+        finish(3, 0, 1, "h0")
         finish(3, 1, 2, "s0")

@@ -27,11 +27,13 @@ ACT_ROW = 64
 E_PLANE = 0
 
 
-def load_scale_rows(queues, plane, first, rows):
-    for q, queue in enumerate(queues):
-        queue.dma_start(
-            out=plane[32 * q + first : 32 * q + first + 4, :].bitcast(I32), in_=rows[0, 4 * q : 4 * q + 4, :].bitcast(I32)
-        )
+def load_scale_rows(nc, table, rows):
+    nc.sync.dma_start(out=table[0:P:8, :].bitcast(I32), in_=rows[0].bitcast(I32))
+
+
+def place_scale_rows(nc, plane, picked):
+    for r in range(4):
+        nc.sync.dma_start(out=plane[r:P:32, :].bitcast(I32), in_=picked[8 * r : P : 32, :].bitcast(I32))
 
 
 def tile_picked_ytani_act_p_kernel(
@@ -48,7 +50,7 @@ def tile_picked_ytani_act_p_kernel(
         xs_tab = keep.tile([P, T], U8, name="xs_tab", align_bytes=64)
         es_tab = keep.tile([P, W], U8, name="es_tab", align_bytes=64)
         qa_tab = keep.tile([P, W], F32, name="qa_tab", align_bytes=64)
-        xw_tab = keep.tile([P, T], U32, name="xw_tab", tag="xw_then_es", align_bytes=64)
+        xw_tab = keep.tile([P, T], U32, name="xw_tab", align_bytes=64)
         ew_tab = keep.tile([P, W], U32, name="ew_tab", align_bytes=64)
         w_raw = [keep.tile([P, PACK, HALF], F32, name="w_raw%d" % u, align_bytes=64) for u in range(2)]
         own_col = [keep.tile([P, 2], F32, name="own_col%d" % u) for u in range(2)]
@@ -58,35 +60,37 @@ def tile_picked_ytani_act_p_kernel(
         warm_in = keep.tile([P, 1], F32, name="warm_in")
         warm_out = keep.tile([P, 1], F32, name="warm_out")
 
+        xs = keep.tile([P, S], U8, name="xs", align_bytes=64)
+        es = keep.tile([P, V], U8, name="es", align_bytes=64)
         nc.vector.memset(xs_tab[:].bitcast(I32), 0)
-        nc.vector.memset(warm_in[:], 1.0)
-        zeros = keep.tile([P, HALF], F32, name="zeros", align_bytes=64)
-        nc.gpsimd.memset(zeros[:], 0.0)
-        nc.vector.tensor_copy(
-            qa_tab[:].rearrange("p (a b) -> p a b", b=HALF), zeros[:].unsqueeze(1).to_broadcast([P, W // HALF, HALF])
-        )
         nc.vector.memset(es_tab[:].bitcast(I32), 0)
+        nc.vector.memset(warm_in[:], 1.0)
+        nc.vector.memset(qa_tab[:], 0.0)
+        nc.vector.memset(xs[:].bitcast(I32), 0)
+        nc.vector.memset(es[:].bitcast(I32), 0)
 
         w_rows = w1.rearrange("(p r) c -> p r c", r=PACK)
         nc.sync.dma_start(offs_sb[:], offs)
         nc.sync.dma_start(refs_sb[:], refs)
-        load_scale_rows((nc.sync, nc.sync, nc.scalar, nc.scalar), xs_tab, 0, x_scales)
         nc.sync.dma_start(out=w_raw[0][:], in_=w_rows[:, :, 0:HALF])
-        nc.sync.dma_start(out=qa_tab[QN_ROW : QN_ROW + 1, :], in_=qn[0:1, :])
-        nc.sync.dma_start(out=qa_tab[ACT_ROW : ACT_ROW + 1, :], in_=act[0:1, :])
+        load_scale_rows(nc, xs_tab, x_scales)
+        load_scale_rows(nc, es_tab, e_scales)
         nc.sync.dma_start(out=w_raw[1][:], in_=w_rows[:, :, HALF : 2 * HALF])
         nc.sync.dma_start(out=own_col[0][:], in_=own_halves[0])
         nc.sync.dma_start(out=xw_tab[:].bitcast(I32), in_=x_words[0].rearrange("p n t -> p (n t)").bitcast(I32))
-        load_scale_rows((nc.sync,) * 4, es_tab, E_PLANE, e_scales)
-        nc.sync.dma_start(out=ew_tab[:].bitcast(I32), in_=e_words[0].rearrange("p n t -> p (n t)").bitcast(I32))
-        nc.sync.dma_start(out=own_late[:, 0:2], in_=own_halves[1])
+        nc.sync.dma_start(out=qa_tab[QN_ROW : QN_ROW + 1, :], in_=qn[0:1, :])
+        nc.sync.dma_start(out=qa_tab[ACT_ROW : ACT_ROW + 1, :], in_=act[0:1, :])
         nc.scalar.activation(warm_out[:], warm_in[:], ACT.Abs_reciprocal_sqrt)
         make_identity(nc, ident[:])
 
-        xs = keep.tile([P, S], U8, name="xs", align_bytes=64)
-        nc.vector.tensor_copy(xs[:], xs_tab[:].indirect(offs_sb[:]))
-        qa = keep.tile([P, V], F32, name="qa", align_bytes=64)
-        nc.vector.tensor_copy(qa[:], qa_tab[:].indirect(refs_sb[:]))
+        xs_picked = keep.tile([P, S], U8, name="xs_picked", align_bytes=64)
+        nc.vector.tensor_copy(xs_picked[:], xs_tab[:].indirect(offs_sb[:]))
+        place_scale_rows(nc, xs, xs_picked)
+        nc.sync.dma_start(out=ew_tab[:].bitcast(I32), in_=e_words[0].rearrange("p n t -> p (n t)").bitcast(I32))
+        nc.sync.dma_start(out=own_late[:, 0:2], in_=own_halves[1])
+        es_picked = keep.tile([P, V], U8, name="es_picked", align_bytes=64)
+        nc.vector.tensor_copy(es_picked[:], es_tab[:].indirect(refs_sb[:]))
+        place_scale_rows(nc, es, es_picked)
 
         w_bf = keep.tile([P, PACK, P, PACK], BF16, name="w_bf", align_bytes=64)
 
@@ -115,11 +119,6 @@ def tile_picked_ytani_act_p_kernel(
             )
 
         spread_own(0, "s0", 1.0 / Y_SCALE)
-        qa_ps = psum.tile([P, NB, P], F32, name="qa_ps", tag="s0")
-        for b in range(NB):
-            nc.tensor.transpose(qa_ps[:, b, :], qa[:, b * P : (b + 1) * P], ident[:])
-        qa_col = keep.tile([P, NB, 2], F32, name="qa_col")
-        nc.scalar.activation(qa_col[:], qa_ps[:, :, QN_ROW : ACT_ROW + 1 : ACT_ROW - QN_ROW], ACT.Copy, scale=1.0 / Y_SCALE)
 
         xq = [
             keep.tile([P, HALF], U32, name="xq0", align_bytes=64),
@@ -127,9 +126,9 @@ def tile_picked_ytani_act_p_kernel(
         ]
         for u in range(2):
             nc.vector.tensor_copy(xq[u][:], xw_tab[:].indirect(offs_sb[:, 16 * u : 16 * (u + 1)]))
-        es = keep.tile([P, V], U8, name="es", tag="xw_then_es", align_bytes=64)
-        nc.vector.tensor_copy(es[:], es_tab[:].indirect(refs_sb[:]))
 
+        qa = keep.tile([P, V], F32, name="qa", align_bytes=64)
+        nc.vector.tensor_copy(qa[:], qa_tab[:].indirect(refs_sb[:]))
         hs = [keep.tile([P, HALF], U8, name="hs%d" % u, align_bytes=64) for u in range(2)]
         h_bf = [keep.tile([P, HALF, PACK], BF16, name="h_bf%d" % u, align_bytes=64) for u in range(2)]
         for c in range(NB):
@@ -146,6 +145,12 @@ def tile_picked_ytani_act_p_kernel(
                     stop=True,
                 )
             nc.scalar.copy(out=h_bf[c // 2][:, cols, :], in_=h_ps[:].rearrange("p j n -> p n j"))
+
+        qa_ps = psum.tile([P, NB, P], F32, name="qa_ps", tag="h1")
+        for b in range(NB):
+            nc.tensor.transpose(qa_ps[:, b, :], qa[:, b * P : (b + 1) * P], ident[:])
+        qa_col = keep.tile([P, NB, 2], F32, name="qa_col")
+        nc.scalar.activation(qa_col[:], qa_ps[:, :, QN_ROW : ACT_ROW + 1 : ACT_ROW - QN_ROW], ACT.Copy, scale=1.0 / Y_SCALE)
 
         def quantize_h(u):
             nc.vector.quantize_mx(out=hq[u][:].bitcast(FP8X4), scales=hs[u][:], in_=h_bf[u][:].rearrange("p n j -> p (n j)"))
@@ -199,8 +204,8 @@ def tile_picked_ytani_act_p_kernel(
                     dneg[n][:, e, :], s_ps[n][e], qa_col[:, 2 * g + e, 0:1], own_row[u][:], ALU.subtract, ALU.subtract
                 )
 
-        def roots(n):
-            nc.scalar.activation(root[n][:], dneg[n][:], ACT.Abs_reciprocal_sqrt)
+        def roots(n, e0=0, e1=2):
+            nc.scalar.activation(root[n][:, e0:e1, :], dneg[n][:, e0:e1, :], ACT.Abs_reciprocal_sqrt)
 
         def squares(n):
             nc.scalar.activation(inv[n][:], root[n][:], ACT.Square)
@@ -233,7 +238,8 @@ def tile_picked_ytani_act_p_kernel(
             product(n)
         for n in range(4):
             denominators(n)
-        roots(0)
+        roots(0, 0, 1)
+        roots(0, 1, 2)
         roots(1)
         squares(0)
         roots(2)

@@ -70,12 +70,12 @@ def tile_picked_ytani_act_p_kernel(
         nc.vector.memset(es[:].bitcast(I32), 0)
 
         w_rows = w1.rearrange("(p r) c -> p r c", r=PACK)
+        nc.sync.dma_start(out=w_raw[0][:], in_=w_rows[:, :, 0:HALF])
         nc.sync.dma_start(offs_sb[:], offs)
         nc.sync.dma_start(refs_sb[:], refs)
-        nc.sync.dma_start(out=w_raw[0][:], in_=w_rows[:, :, 0:HALF])
         load_scale_rows(nc, xs_tab, x_scales)
-        load_scale_rows(nc, es_tab, e_scales)
         nc.sync.dma_start(out=w_raw[1][:], in_=w_rows[:, :, HALF : 2 * HALF])
+        load_scale_rows(nc, es_tab, e_scales)
         nc.sync.dma_start(out=own_col[0][:], in_=own_halves[0])
         nc.sync.dma_start(out=xw_tab[:].bitcast(I32), in_=x_words[0].rearrange("p n t -> p (n t)").bitcast(I32))
         nc.sync.dma_start(out=qa_tab[QN_ROW : QN_ROW + 1, :], in_=qn[0:1, :])

@@ -22,6 +22,7 @@ PACK = 4
 NB = 4
 HALF = 256
 Y_SCALE = 0.3
+TINY = 2.0**-60
 QN_ROW = 0
 ACT_ROW = 64
 E_PLANE = 0
@@ -65,7 +66,9 @@ def tile_picked_ytani_act_p_kernel(
         nc.vector.memset(xs_tab[:].bitcast(I32), 0)
         nc.vector.memset(es_tab[:].bitcast(I32), 0)
         nc.vector.memset(warm_in[:], 1.0)
-        nc.vector.memset(qa_tab[:], 0.0)
+        nc.vector.memset(qa_tab[:, 0 : W // 2], 0.0)
+        make_identity(nc, ident[:])
+        nc.gpsimd.memset(qa_tab[:, W // 2 : W], 0.0)
         nc.vector.memset(xs[:].bitcast(I32), 0)
         nc.vector.memset(es[:].bitcast(I32), 0)
 
@@ -81,7 +84,6 @@ def tile_picked_ytani_act_p_kernel(
         nc.sync.dma_start(out=qa_tab[QN_ROW : QN_ROW + 1, :], in_=qn[0:1, :])
         nc.sync.dma_start(out=qa_tab[ACT_ROW : ACT_ROW + 1, :], in_=act[0:1, :])
         nc.scalar.activation(warm_out[:], warm_in[:], ACT.Abs_reciprocal_sqrt)
-        make_identity(nc, ident[:])
 
         xs_picked = keep.tile([P, S], U8, name="xs_picked", align_bytes=64)
         nc.vector.tensor_copy(xs_picked[:], xs_tab[:].indirect(offs_sb[:]))
@@ -210,8 +212,9 @@ def tile_picked_ytani_act_p_kernel(
         def squares(n):
             nc.scalar.activation(inv[n][:], root[n][:], ACT.Square)
 
-        def half_sign(n):
-            nc.vector.tensor_scalar(sgn[n][:], dneg[n][:], 0.0, 0.5, ALU.is_gt, ALU.subtract)
+        def tiny_sign(n):
+            engine = nc.gpsimd if n < 2 else nc.vector
+            engine.tensor_scalar(sgn[n][:], dneg[n][:], TINY, -TINY, ALU.min, ALU.max)
 
         def scale_sums(n, e):
             g = quads[n][1]
@@ -230,7 +233,7 @@ def tile_picked_ytani_act_p_kernel(
                 for e in range(2):
                     nc.tensor.transpose(o_ps[:, c - c0, e * P : (e + 1) * P], arg[n][:, e, c * P : (c + 1) * P], ident[:])
             res = keep.tile([P, c1 - c0, HALF], F32, name="res%d_%d" % (n, c0), align_bytes=64)
-            nc.scalar.activation(res[:], o_ps[:], ACT.Tanh, scale=-2.0 * Y_SCALE)
+            nc.scalar.activation(res[:], o_ps[:], ACT.Tanh, scale=-Y_SCALE / TINY)
             rows = slice(u * HALF + c0 * P, u * HALF + c1 * P)
             nc.sync.dma_start(out=out[rows, g * HALF : (g + 1) * HALF].rearrange("(c p) v -> p c v", p=P), in_=res[:])
 
@@ -238,32 +241,27 @@ def tile_picked_ytani_act_p_kernel(
             product(n)
         for n in range(4):
             denominators(n)
+        tiny_sign(0)
+        tiny_sign(1)
         roots(0, 0, 1)
         roots(0, 1, 2)
         roots(1)
-        squares(0)
+        nc.vector.tensor_tensor(inv[0][:, 0, :], root[0][:, 0, :], root[0][:, 0, :], ALU.mult)
+        nc.scalar.activation(inv[0][:, 1, :], root[0][:, 1, :], ACT.Square)
         roots(2)
-        squares(1)
         roots(3)
-        squares(2)
-        squares(3)
-        half_sign(0)
-        half_sign(1)
-        scale_sums(0, 0)
-        scale_sums(0, 1)
-        half_sign(2)
-        apply_sign(0, 0, 2)
-        finish(0, 0, 2, "h1")
-        scale_sums(1, 0)
-        scale_sums(1, 1)
-        half_sign(3)
-        apply_sign(1, 0, 2)
-        finish(1, 0, 2, "h2")
-        scale_sums(2, 0)
-        scale_sums(2, 1)
+        for n in range(1, 4):
+            squares(n)
+        tiny_sign(2)
+        for n, bank in enumerate(("h1", "h2", "h3")):
+            scale_sums(n, 0)
+            scale_sums(n, 1)
+            apply_sign(n, 0, 1)
+            apply_sign(n, 1, 2)
+            finish(n, 0, 2, bank)
+            if n == 0:
+                tiny_sign(3)
         scale_sums(3, 0)
-        apply_sign(2, 0, 2)
-        finish(2, 0, 2, "h3")
         scale_sums(3, 1)
         apply_sign(3, 0, 1)
         apply_sign(3, 1, 2, 0, 1)

@@ -25,7 +25,6 @@ Y_SCALE = 0.3
 TINY = 2.0**-60
 QN_ROW = 0
 ACT_ROW = 64
-E_PLANE = 0
 
 
 def load_scale_rows(nc, table, rows):
@@ -173,98 +172,102 @@ def tile_picked_ytani_act_p_kernel(
         quantize_h(1)
         spread_own(1, "s3", 1.0)
 
-        quads = [(u, g) for u in range(2) for g in range(2)]
-        s_ps, dneg, root, inv, sgn, num, arg = [], [], [], [], [], [], []
-        for n in range(len(quads)):
-            for group, label in ((dneg, "dneg"), (root, "root"), (inv, "inv"), (sgn, "sgn"), (num, "num"), (arg, "arg")):
-                group.append(keep.tile([P, 2, HALF], F32, name="%s%d" % (label, n), align_bytes=64))
+        s_ps, dneg, root, sgn = {}, {}, {}, {}
+        for u in range(2):
+            for g in range(2):
+                for group, label in ((dneg, "dneg"), (root, "root"), (sgn, "sgn")):
+                    group[u, g] = keep.tile([P, 2, HALF], F32, name="%s%d%d" % (label, u, g), align_bytes=64)
+        num = []
+        inv = [keep.tile([P, NB, HALF], F32, name="inv%d" % u, align_bytes=64) for u in range(2)]
+        arg = [keep.tile([P, NB, HALF], F32, name="arg%d" % u, align_bytes=64) for u in range(2)]
 
-        def product(n):
-            u, g = quads[n]
-            if n == 0:
+        def product(u, g):
+            if (u, g) == (0, 0):
                 sp = [psum.tile([P, HALF], F32, name="s_ps0_%d" % e, tag=bank)[:] for e, bank in enumerate(("h0", "s0"))]
             else:
-                both = psum.tile([P, 2, HALF], F32, name="s_ps%d" % n, tag="s%d" % n)
+                both = psum.tile([P, 2, HALF], F32, name="s_ps%d%d" % (u, g), tag="s%d" % (2 * u + g))
                 sp = [both[:, e, :] for e in range(2)]
             for e in range(2):
                 b = 2 * g + e
                 nc.tensor.matmul_mx(
                     out=sp[e],
                     lhsT=eq[g][:, e * P : (e + 1) * P].bitcast(FP8X4),
-                    lhsT_scale=es[E_PLANE:P, b * P : (b + 1) * P],
+                    lhsT_scale=es[:, b * P : (b + 1) * P],
                     rhs=hq[u][:].bitcast(FP8X4),
                     rhs_scale=hs[u][:],
                     start=True,
                     stop=True,
                 )
-            s_ps.append(sp)
+            s_ps[u, g] = sp
 
-        def denominators(n):
-            u, g = quads[n]
+        def denominators(u, g):
             for e in range(2):
+                qn_col = qa_col[:, 2 * g + e, 0:1]
+                nc.vector.scalar_tensor_tensor(dneg[u, g][:, e, :], s_ps[u, g][e], qn_col, own_row[u][:], ALU.subtract, ALU.subtract)
+            nc.gpsimd.tensor_scalar(sgn[u, g][:], dneg[u, g][:], TINY, -TINY, ALU.min, ALU.max)
+
+        def roots(u, g, e0=0, e1=2):
+            nc.scalar.activation(root[u, g][:, e0:e1, :], dneg[u, g][:, e0:e1, :], ACT.Abs_reciprocal_sqrt)
+
+        def squares(u, g):
+            nc.scalar.activation(inv[u][:, 2 * g : 2 * g + 2, :], root[u, g][:], ACT.Square)
+
+        def numerators(u, g):
+            for e in range(2):
+                b = 2 * g + e
                 nc.vector.scalar_tensor_tensor(
-                    dneg[n][:, e, :], s_ps[n][e], qa_col[:, 2 * g + e, 0:1], own_row[u][:], ALU.subtract, ALU.subtract
+                    num[u][:, b, :], s_ps[u, g][e], qa_col[:, b, 1:2], sgn[u, g][:, e, :], ALU.mult, ALU.mult
                 )
 
-        def roots(n, e0=0, e1=2):
-            nc.scalar.activation(root[n][:, e0:e1, :], dneg[n][:, e0:e1, :], ACT.Abs_reciprocal_sqrt)
+        def quotients(u, c, b0, b1):
+            cols = slice(c * P, (c + 1) * P)
+            nc.vector.tensor_tensor(arg[u][:, b0:b1, cols], num[u][:, b0:b1, cols], inv[u][:, b0:b1, cols], ALU.mult)
 
-        def squares(n):
-            nc.scalar.activation(inv[n][:], root[n][:], ACT.Square)
-
-        def tiny_sign(n):
-            engine = nc.gpsimd if n < 2 else nc.vector
-            engine.tensor_scalar(sgn[n][:], dneg[n][:], TINY, -TINY, ALU.min, ALU.max)
-
-        def scale_sums(n, e):
-            g = quads[n][1]
-            nc.vector.scalar_tensor_tensor(
-                num[n][:, e, :], s_ps[n][e], qa_col[:, 2 * g + e, 1:2], inv[n][:, e, :], ALU.mult, ALU.mult
-            )
-
-        def apply_sign(n, e0, e1, c0=0, c1=2):
-            cols = slice(c0 * P, c1 * P)
-            nc.vector.tensor_tensor(arg[n][:, e0:e1, cols], num[n][:, e0:e1, cols], sgn[n][:, e0:e1, cols], ALU.mult)
-
-        def finish(n, c0, c1, bank):
-            u, g = quads[n]
-            o_ps = psum.tile([P, c1 - c0, HALF], F32, name="o_ps%d_%d" % (n, c0), tag=bank)
-            for c in range(c0, c1):
-                for e in range(2):
-                    nc.tensor.transpose(o_ps[:, c - c0, e * P : (e + 1) * P], arg[n][:, e, c * P : (c + 1) * P], ident[:])
-            res = keep.tile([P, c1 - c0, HALF], F32, name="res%d_%d" % (n, c0), align_bytes=64)
+        def finish(u, c, b0, b1, bank, tag=None):
+            cols = slice(c * P, (c + 1) * P)
+            name = "%d%d%d" % (u, c, b0)
+            o_ps = psum.tile([P, b1 - b0, P], F32, name="o_ps" + name, tag=bank)
+            for b in range(b0, b1):
+                nc.tensor.transpose(o_ps[:, b - b0, :], arg[u][:, b, cols], ident[:])
+            res = keep.tile([P, b1 - b0, P], F32, name="res" + name, tag=tag or "res" + name, align_bytes=64)
             nc.scalar.activation(res[:], o_ps[:], ACT.Tanh, scale=-Y_SCALE / TINY)
-            rows = slice(u * HALF + c0 * P, u * HALF + c1 * P)
-            nc.sync.dma_start(out=out[rows, g * HALF : (g + 1) * HALF].rearrange("(c p) v -> p c v", p=P), in_=res[:])
+            rows = slice(u * HALF + c * P, u * HALF + (c + 1) * P)
+            nc.sync.dma_start(out=out[rows, b0 * P : b1 * P], in_=res[:].rearrange("p b v -> p (b v)"))
 
-        for n in range(4):
-            product(n)
-        for n in range(4):
-            denominators(n)
-        tiny_sign(0)
-        tiny_sign(1)
-        roots(0, 0, 1)
-        roots(0, 1, 2)
-        roots(1)
-        nc.vector.tensor_tensor(inv[0][:, 0, :], root[0][:, 0, :], root[0][:, 0, :], ALU.mult)
-        nc.scalar.activation(inv[0][:, 1, :], root[0][:, 1, :], ACT.Square)
-        roots(2)
-        roots(3)
-        for n in range(1, 4):
-            squares(n)
-        tiny_sign(2)
-        for n, bank in enumerate(("h1", "h2", "h3")):
-            scale_sums(n, 0)
-            scale_sums(n, 1)
-            apply_sign(n, 0, 1)
-            apply_sign(n, 1, 2)
-            finish(n, 0, 2, bank)
-            if n == 0:
-                tiny_sign(3)
-        scale_sums(3, 0)
-        scale_sums(3, 1)
-        apply_sign(3, 0, 1)
-        apply_sign(3, 1, 2, 0, 1)
-        apply_sign(3, 1, 2, 1, 2)
-        finish(3, 0, 1, "h0")
-        finish(3, 1, 2, "s0")
+        product(0, 0)
+        product(0, 1)
+        denominators(0, 0)
+        product(1, 0)
+        product(1, 1)
+        denominators(0, 1)
+        roots(0, 0, 0, 1)
+        roots(0, 0, 1, 2)
+        squares(0, 0)
+        roots(0, 1)
+        squares(0, 1)
+        denominators(1, 0)
+        denominators(1, 1)
+        roots(1, 0)
+        roots(1, 1)
+        squares(1, 0)
+        squares(1, 1)
+        tanh_warm = keep.tile([P, 1], F32, name="tanh_warm")
+        nc.scalar.activation(tanh_warm[:], root[1, 1][:, 1, 0:1], ACT.Tanh)
+        num.append(keep.tile([P, NB, HALF], F32, name="num0", tag="own_row1", align_bytes=64))
+        num.append(keep.tile([P, NB, HALF], F32, name="num1", align_bytes=64))
+        numerators(0, 0)
+        numerators(0, 1)
+        quotients(0, 0, 0, 4)
+        finish(0, 0, 0, 4, "h1", "dneg11")
+        numerators(1, 0)
+        quotients(0, 1, 0, 4)
+        finish(0, 1, 0, 4, "h2")
+        numerators(1, 1)
+        quotients(1, 0, 0, 2)
+        quotients(1, 0, 2, 4)
+        finish(1, 0, 0, 4, "h3")
+        quotients(1, 1, 0, 2)
+        finish(1, 1, 0, 2, "h0")
+        quotients(1, 1, 2, 3)
+        quotients(1, 1, 3, 4)
+        finish(1, 1, 2, 4, "s0")

@@ -33,7 +33,7 @@ def load_scale_rows(nc, table, rows):
 
 def place_scale_rows(nc, plane, picked):
     for r in range(4):
-        nc.sync.dma_start(out=plane[r:P:32, :].bitcast(I32), in_=picked[8 * r : P : 32, :].bitcast(I32))
+        nc.sync.dma_start(out=plane[r:P:32, :].bitcast(I32), in_=picked[8 * r : P : 32, 0:V].bitcast(I32))
 
 
 def tile_picked_ytani_act_p_kernel(
@@ -53,9 +53,7 @@ def tile_picked_ytani_act_p_kernel(
         xw_tab = keep.tile([P, T], U32, name="xw_tab", align_bytes=64)
         ew_tab = keep.tile([P, W], U32, name="ew_tab", align_bytes=64)
         w_raw = [keep.tile([P, PACK, HALF], F32, name="w_raw%d" % u, align_bytes=64) for u in range(2)]
-        own_col = [keep.tile([P, 2], F32, name="own_col%d" % u) for u in range(2)]
-        own_late = late.tile([P, HALF + 32], F32, name="own_late", offset=4 * HALF - 64, align_bytes=64)
-        own_halves = own.rearrange("(u p c) o -> u p (c o)", u=2, c=2)
+        own_col = keep.tile([P, PACK], F32, name="own_col")
         ident = keep.tile([P, P], F32, name="ident", align_bytes=64)
         warm_in = keep.tile([P, 1], F32, name="warm_in")
         warm_out = keep.tile([P, 1], F32, name="warm_out")
@@ -78,7 +76,7 @@ def tile_picked_ytani_act_p_kernel(
         load_scale_rows(nc, xs_tab, x_scales)
         nc.sync.dma_start(out=w_raw[1][:], in_=w_rows[:, :, HALF : 2 * HALF])
         load_scale_rows(nc, es_tab, e_scales)
-        nc.sync.dma_start(out=own_col[0][:], in_=own_halves[0])
+        nc.sync.dma_start(out=own_col[:], in_=own.rearrange("(p c) o -> p (c o)", c=PACK))
         nc.sync.dma_start(out=xw_tab[:].bitcast(I32), in_=x_words[0].rearrange("p n t -> p (n t)").bitcast(I32))
         nc.sync.dma_start(out=qa_tab[QN_ROW : QN_ROW + 1, :], in_=qn[0:1, :])
         nc.sync.dma_start(out=qa_tab[ACT_ROW : ACT_ROW + 1, :], in_=act[0:1, :])
@@ -88,9 +86,8 @@ def tile_picked_ytani_act_p_kernel(
         nc.vector.tensor_copy(xs_picked[:], xs_tab[:].indirect(offs_sb[:]))
         place_scale_rows(nc, xs, xs_picked)
         nc.sync.dma_start(out=ew_tab[:].bitcast(I32), in_=e_words[0].rearrange("p n t -> p (n t)").bitcast(I32))
-        nc.sync.dma_start(out=own_late[:, 0:2], in_=own_halves[1])
-        es_picked = keep.tile([P, V], U8, name="es_picked", align_bytes=64)
-        nc.vector.tensor_copy(es_picked[:], es_tab[:].indirect(refs_sb[:]))
+        es_picked = late.tile([P, 4 * HALF + 128], U8, name="es_picked", offset=4 * HALF - 64, align_bytes=64)
+        nc.vector.tensor_copy(es_picked[:, 0:V], es_tab[:].indirect(refs_sb[:]))
         place_scale_rows(nc, es, es_picked)
 
         w_bf = keep.tile([P, PACK, P, PACK], BF16, name="w_bf", align_bytes=64)
@@ -111,15 +108,16 @@ def tile_picked_ytani_act_p_kernel(
 
         own_row = [keep.tile([P, HALF], F32, name="own_row%d" % u, align_bytes=64) for u in range(2)]
 
-        def spread_own(u, bank, scale):
-            own_ps = psum.tile([P, 2, P], F32, name="own_ps%d" % u, tag=bank)
-            for c in range(2):
-                nc.tensor.transpose(own_ps[:, c, :], own_col[u][:, c : c + 1].to_broadcast([P, P]), ident[:])
+        own_ps = psum.tile([P, PACK, P], F32, name="own_ps", tag="s3")
+        for c in range(PACK):
+            nc.tensor.transpose(own_ps[:, c, :], own_col[:, c : c + 1].to_broadcast([P, P]), ident[:])
+        for u in range(2):
             nc.scalar.activation(
-                own_row[u][:].rearrange("p (n c) -> p n c", c=2), own_ps[:].rearrange("p c n -> p n c"), ACT.Copy, scale=scale
+                own_row[u][:].rearrange("p (n c) -> p n c", c=PACK),
+                own_ps[:, :, u * 64 : (u + 1) * 64].rearrange("p c n -> p n c"),
+                ACT.Copy,
+                scale=1.0 / Y_SCALE,
             )
-
-        spread_own(0, "s0", 1.0 / Y_SCALE)
 
         xq = [
             keep.tile([P, HALF], U32, name="xq0", align_bytes=64),
@@ -161,7 +159,6 @@ def tile_picked_ytani_act_p_kernel(
 
         eq = [keep.tile([P, HALF], U32, name="eq0", align_bytes=64)]
         gather_e(0)
-        nc.vector.tensor_scalar_mul(own_col[1][:], own_late[:, 0:2], 1.0 / Y_SCALE)
         hq = [
             late.tile([P, HALF], U32, name="hq0", offset=0, align_bytes=64),
             late.tile([P, HALF], U32, name="hq1", offset=8 * HALF, align_bytes=64),
@@ -170,16 +167,12 @@ def tile_picked_ytani_act_p_kernel(
         quantize_h(0)
         gather_e(1)
         quantize_h(1)
-        spread_own(1, "s3", 1.0)
 
-        s_ps, dneg, root, sgn = {}, {}, {}, {}
+        s_ps, dneg, root, sgn, num, inv, arg = {}, {}, {}, {}, {}, {}, {}
         for u in range(2):
             for g in range(2):
-                for group, label in ((dneg, "dneg"), (root, "root"), (sgn, "sgn")):
+                for group, label in ((dneg, "dneg"), (root, "root"), (sgn, "sgn"), (arg, "arg")):
                     group[u, g] = keep.tile([P, 2, HALF], F32, name="%s%d%d" % (label, u, g), align_bytes=64)
-        num = []
-        inv = [keep.tile([P, NB, HALF], F32, name="inv%d" % u, align_bytes=64) for u in range(2)]
-        arg = [keep.tile([P, NB, HALF], F32, name="arg%d" % u, align_bytes=64) for u in range(2)]
 
         def product(u, g):
             if (u, g) == (0, 0):
@@ -209,30 +202,33 @@ def tile_picked_ytani_act_p_kernel(
         def roots(u, g, e0=0, e1=2):
             nc.scalar.activation(root[u, g][:, e0:e1, :], dneg[u, g][:, e0:e1, :], ACT.Abs_reciprocal_sqrt)
 
-        def squares(u, g):
-            nc.scalar.activation(inv[u][:, 2 * g : 2 * g + 2, :], root[u, g][:], ACT.Square)
+        def squares(u, g, step=2):
+            inv[u, g] = keep.tile([P, 2, HALF], F32, name="inv%d%d" % (u, g), align_bytes=64)
+            for e in range(0, 2, step):
+                nc.scalar.activation(inv[u, g][:, e : e + step, :], root[u, g][:, e : e + step, :], ACT.Square)
 
-        def numerators(u, g):
+        def numerators(u, g, tag=None):
+            name = "num%d%d" % (u, g)
+            num[u, g] = keep.tile([P, 2, HALF], F32, name=name, tag=tag or name, align_bytes=64)
             for e in range(2):
-                b = 2 * g + e
                 nc.vector.scalar_tensor_tensor(
-                    num[u][:, b, :], s_ps[u, g][e], qa_col[:, b, 1:2], sgn[u, g][:, e, :], ALU.mult, ALU.mult
+                    num[u, g][:, e, :], s_ps[u, g][e], qa_col[:, 2 * g + e, 1:2], sgn[u, g][:, e, :], ALU.mult, ALU.mult
                 )
 
-        def quotients(u, c, b0, b1):
-            cols = slice(c * P, (c + 1) * P)
-            nc.vector.tensor_tensor(arg[u][:, b0:b1, cols], num[u][:, b0:b1, cols], inv[u][:, b0:b1, cols], ALU.mult)
+        def quotients(u, g, c0, c1, e0=0, e1=2):
+            cols = slice(c0 * P, c1 * P)
+            nc.vector.tensor_tensor(arg[u, g][:, e0:e1, cols], num[u, g][:, e0:e1, cols], inv[u, g][:, e0:e1, cols], ALU.mult)
 
-        def finish(u, c, b0, b1, bank, tag=None):
-            cols = slice(c * P, (c + 1) * P)
-            name = "%d%d%d" % (u, c, b0)
-            o_ps = psum.tile([P, b1 - b0, P], F32, name="o_ps" + name, tag=bank)
-            for b in range(b0, b1):
-                nc.tensor.transpose(o_ps[:, b - b0, :], arg[u][:, b, cols], ident[:])
-            res = keep.tile([P, b1 - b0, P], F32, name="res" + name, tag=tag or "res" + name, align_bytes=64)
+        def finish(u, g, c0, c1, bank, tag=None):
+            name = "%d%d%d" % (u, g, c0)
+            o_ps = psum.tile([P, c1 - c0, HALF], F32, name="o_ps" + name, tag=bank)
+            for c in range(c0, c1):
+                for e in range(2):
+                    nc.tensor.transpose(o_ps[:, c - c0, e * P : (e + 1) * P], arg[u, g][:, e, c * P : (c + 1) * P], ident[:])
+            res = keep.tile([P, c1 - c0, HALF], F32, name="res" + name, tag=tag or "res" + name, align_bytes=64)
             nc.scalar.activation(res[:], o_ps[:], ACT.Tanh, scale=-Y_SCALE / TINY)
-            rows = slice(u * HALF + c * P, u * HALF + (c + 1) * P)
-            nc.sync.dma_start(out=out[rows, b0 * P : b1 * P], in_=res[:].rearrange("p b v -> p (b v)"))
+            rows = slice(u * HALF + c0 * P, u * HALF + c1 * P)
+            nc.sync.dma_start(out=out[rows, g * HALF : (g + 1) * HALF].rearrange("(c p) v -> p c v", p=P), in_=res[:])
 
         product(0, 0)
         product(0, 1)
@@ -242,7 +238,7 @@ def tile_picked_ytani_act_p_kernel(
         denominators(0, 1)
         roots(0, 0, 0, 1)
         roots(0, 0, 1, 2)
-        squares(0, 0)
+        squares(0, 0, 1)
         roots(0, 1)
         squares(0, 1)
         denominators(1, 0)
@@ -250,24 +246,24 @@ def tile_picked_ytani_act_p_kernel(
         roots(1, 0)
         roots(1, 1)
         squares(1, 0)
-        squares(1, 1)
         tanh_warm = keep.tile([P, 1], F32, name="tanh_warm")
         nc.scalar.activation(tanh_warm[:], root[1, 1][:, 1, 0:1], ACT.Tanh)
-        num.append(keep.tile([P, NB, HALF], F32, name="num0", tag="own_row1", align_bytes=64))
-        num.append(keep.tile([P, NB, HALF], F32, name="num1", align_bytes=64))
-        numerators(0, 0)
-        numerators(0, 1)
-        quotients(0, 0, 0, 4)
-        finish(0, 0, 0, 4, "h1", "dneg11")
+        numerators(0, 0, "own_row1")
+        numerators(0, 1, "num01")
+        quotients(0, 0, 0, 2)
+        finish(0, 0, 0, 2, "h1", "dneg11")
+        quotients(0, 1, 0, 2)
+        finish(0, 1, 0, 2, "h2")
         numerators(1, 0)
-        quotients(0, 1, 0, 4)
-        finish(0, 1, 0, 4, "h2")
+        inv[1, 1] = keep.tile([P, 2, HALF], F32, name="inv11", align_bytes=64)
+        nc.vector.tensor_tensor(inv[1, 1][:], root[1, 1][:], root[1, 1][:], ALU.mult)
+        quotients(1, 0, 0, 1)
+        finish(1, 0, 0, 1, "h3")
         numerators(1, 1)
-        quotients(1, 0, 0, 2)
-        quotients(1, 0, 2, 4)
-        finish(1, 0, 0, 4, "h3")
-        quotients(1, 1, 0, 2)
-        finish(1, 1, 0, 2, "h0")
-        quotients(1, 1, 2, 3)
-        quotients(1, 1, 3, 4)
-        finish(1, 1, 2, 4, "s0")
+        quotients(1, 0, 1, 2)
+        finish(1, 0, 1, 2, "h0")
+        quotients(1, 1, 0, 1)
+        finish(1, 1, 0, 1, "s0")
+        quotients(1, 1, 1, 2, 0, 1)
+        quotients(1, 1, 1, 2, 1, 2)
+        finish(1, 1, 1, 2, "s1")

@@ -63,9 +63,8 @@ def tile_picked_ytani_act_p_kernel(
         nc.vector.memset(xs_tab[:].bitcast(I32), 0)
         nc.vector.memset(es_tab[:].bitcast(I32), 0)
         nc.vector.memset(warm_in[:], 1.0)
-        nc.vector.memset(qa_tab[:, 0 : W // 2], 0.0)
+        nc.vector.memset(qa_tab[:], 0.0)
         make_identity(nc, ident[:])
-        nc.gpsimd.memset(qa_tab[:, W // 2 : W], 0.0)
         nc.vector.memset(xs[:].bitcast(I32), 0)
         nc.vector.memset(es[:].bitcast(I32), 0)
 

@@ -23,6 +23,7 @@ NB = 4
 HALF = 256
 Y_SCALE = 0.3
 TINY = 2.0**-60
+SQ_SCALAR = 64
 QN_ROW = 0
 ACT_ROW = 64
 
@@ -206,12 +207,14 @@ def tile_picked_ytani_act_p_kernel(
             for e in range(0, 2, step):
                 nc.scalar.activation(inv[u, g][:, e : e + step, :], root[u, g][:, e : e + step, :], ACT.Square)
 
-        def numerators(u, g, tag=None):
+        def numerators(u, g, tag=None, c0=0, c1=2):
             name = "num%d%d" % (u, g)
-            num[u, g] = keep.tile([P, 2, HALF], F32, name=name, tag=tag or name, align_bytes=64)
+            if c0 == 0:
+                num[u, g] = keep.tile([P, 2, HALF], F32, name=name, tag=tag or name, align_bytes=64)
+            cols = slice(c0 * P, c1 * P)
             for e in range(2):
                 nc.vector.scalar_tensor_tensor(
-                    num[u, g][:, e, :], s_ps[u, g][e], qa_col[:, 2 * g + e, 1:2], sgn[u, g][:, e, :], ALU.mult, ALU.mult
+                    num[u, g][:, e, cols], s_ps[u, g][e][:, cols], qa_col[:, 2 * g + e, 1:2], sgn[u, g][:, e, cols], ALU.mult, ALU.mult
                 )
 
         def quotients(u, g, c0, c1, e0=0, e1=2):
@@ -225,9 +228,10 @@ def tile_picked_ytani_act_p_kernel(
                 for e in range(2):
                     nc.tensor.transpose(o_ps[:, c - c0, e * P : (e + 1) * P], arg[u, g][:, e, c * P : (c + 1) * P], ident[:])
             res = keep.tile([P, c1 - c0, HALF], F32, name="res" + name, tag=tag or "res" + name, align_bytes=64)
-            nc.scalar.activation(res[:], o_ps[:], ACT.Tanh, scale=-Y_SCALE / TINY)
-            rows = slice(u * HALF + c0 * P, u * HALF + c1 * P)
-            nc.sync.dma_start(out=out[rows, g * HALF : (g + 1) * HALF].rearrange("(c p) v -> p c v", p=P), in_=res[:])
+            for c in range(c0, c1):
+                nc.scalar.activation(res[:, c - c0, :], o_ps[:, c - c0, :], ACT.Tanh, scale=-Y_SCALE / TINY)
+                rows = slice(u * HALF + c * P, u * HALF + (c + 1) * P)
+                nc.sync.dma_start(out=out[rows, g * HALF : (g + 1) * HALF], in_=res[:, c - c0, :])
 
         product(0, 0)
         product(0, 1)
@@ -245,24 +249,33 @@ def tile_picked_ytani_act_p_kernel(
         roots(1, 0)
         roots(1, 1)
         squares(1, 0)
+        inv[1, 1] = keep.tile([P, 2, HALF], F32, name="inv11", align_bytes=64)
+        nc.scalar.activation(inv[1, 1][:, :, 0:SQ_SCALAR], root[1, 1][:, :, 0:SQ_SCALAR], ACT.Square)
         tanh_warm = keep.tile([P, 1], F32, name="tanh_warm")
         nc.scalar.activation(tanh_warm[:], root[1, 1][:, 1, 0:1], ACT.Tanh)
         numerators(0, 0, "own_row1")
         numerators(0, 1, "num01")
         quotients(0, 0, 0, 2)
-        finish(0, 0, 0, 2, "h1", "dneg11")
+        finish(0, 0, 0, 1, "h1", "dneg11")
+        finish(0, 0, 1, 2, "h2")
         quotients(0, 1, 0, 2)
-        finish(0, 1, 0, 2, "h2")
+        finish(0, 1, 0, 1, "h3")
+        finish(0, 1, 1, 2, "h0")
         numerators(1, 0)
-        inv[1, 1] = keep.tile([P, 2, HALF], F32, name="inv11", align_bytes=64)
-        nc.vector.tensor_tensor(inv[1, 1][:], root[1, 1][:], root[1, 1][:], ALU.mult)
+        nc.vector.tensor_tensor(inv[1, 1][:, :, SQ_SCALAR:], root[1, 1][:, :, SQ_SCALAR:], root[1, 1][:, :, SQ_SCALAR:], ALU.mult)
+        numerators(1, 1, None, 0, 1)
         quotients(1, 0, 0, 1)
-        finish(1, 0, 0, 1, "h3")
-        numerators(1, 1)
+        finish(1, 0, 0, 1, "s0")
         quotients(1, 0, 1, 2)
-        finish(1, 0, 1, 2, "h0")
+        finish(1, 0, 1, 2, "s1")
         quotients(1, 1, 0, 1)
-        finish(1, 1, 0, 1, "s0")
+        finish(1, 1, 0, 1, "s2")
+        numerators(1, 1, None, 1, 2)
         quotients(1, 1, 1, 2, 0, 1)
         quotients(1, 1, 1, 2, 1, 2)
-        finish(1, 1, 1, 2, "s1")
+        last = keep.tile([P, HALF], F32, name="res_last", align_bytes=64)
+        for e, bank in enumerate(("h1", "h2")):
+            o_ps = psum.tile([P, P], F32, name="o_ps_last%d" % e, tag=bank)
+            nc.tensor.transpose(o_ps[:], arg[1, 1][:, e, P:HALF], ident[:])
+            nc.scalar.activation(last[:, e * P : (e + 1) * P], o_ps[:], ACT.Tanh, scale=-Y_SCALE / TINY)
+        nc.sync.dma_start(out=out[HALF + P : S, HALF:V], in_=last[:])

@@ -278,4 +278,4 @@ def tile_picked_ytani_act_p_kernel(
             o_ps = psum.tile([P, P], F32, name="o_ps_last%d" % e, tag=bank)
             nc.tensor.transpose(o_ps[:], arg[1, 1][:, e, P:HALF], ident[:])
             nc.scalar.activation(last[:, e * P : (e + 1) * P], o_ps[:], ACT.Tanh, scale=-Y_SCALE / TINY)
-        nc.sync.dma_start(out=out[HALF + P : S, HALF:V], in_=last[:])
+        nc.scalar.dma_start(out=out[HALF + P : S, HALF:V], in_=last[:])

@@ -23,9 +23,9 @@ NB = 4
 HALF = 256
 Y_SCALE = 0.3
 TINY = 2.0**-60
-SQ_SCALAR = 64
 QN_ROW = 0
 ACT_ROW = 64
+W_SCALAR_END = 96
 
 
 def load_scale_rows(nc, table, rows):
@@ -46,21 +46,24 @@ def tile_picked_ytani_act_p_kernel(
         late = ctx.enter_context(tc.tile_pool(name="late", bufs=1))
         psum = ctx.enter_context(tc.psum_pool(name="psum", bufs=1))
 
+        def tile(name, shape, dtype, tag=None):
+            return keep.tile(shape, dtype, name=name, tag=tag or name, align_bytes=64)
+
         offs_sb = keep.tile([P, S // 16], U16, name="offs_sb")
         refs_sb = keep.tile([P, V // 16], U16, name="refs_sb")
-        xs_tab = keep.tile([P, T], U8, name="xs_tab", align_bytes=64)
-        es_tab = keep.tile([P, W], U8, name="es_tab", align_bytes=64)
-        qa_tab = keep.tile([P, W], F32, name="qa_tab", align_bytes=64)
-        xw_tab = keep.tile([P, T], U32, name="xw_tab", align_bytes=64)
-        ew_tab = keep.tile([P, W], U32, name="ew_tab", align_bytes=64)
-        w_raw = [keep.tile([P, PACK, HALF], F32, name="w_raw%d" % u, align_bytes=64) for u in range(2)]
-        own_col = keep.tile([P, PACK], F32, name="own_col")
-        ident = keep.tile([P, P], F32, name="ident", align_bytes=64)
-        warm_in = keep.tile([P, 1], F32, name="warm_in")
-        warm_out = keep.tile([P, 1], F32, name="warm_out")
+        xs_tab = tile("xs_tab", [P, T], U8)
+        es_tab = tile("es_tab", [P, W], U8)
+        qa_tab = tile("qa_tab", [P, W], F32)
+        xw_tab = tile("xw_tab", [P, T], U32)
+        ew_tab = tile("ew_tab", [P, W], U32)
+        w_raw = [tile("w_raw%d" % u, [P, PACK, HALF], F32) for u in range(2)]
+        own_col = tile("own_col", [P, PACK], F32)
+        ident = tile("ident", [P, P], F32)
+        warm_in = tile("warm_in", [P, 1], F32)
+        warm_out = tile("warm_out", [P, 1], F32)
+        xs = tile("xs", [P, S], U8)
+        es = tile("es", [P, V], U8)
 
-        xs = keep.tile([P, S], U8, name="xs", align_bytes=64)
-        es = keep.tile([P, V], U8, name="es", align_bytes=64)
         nc.vector.memset(xs_tab[:].bitcast(I32), 0)
         nc.vector.memset(es_tab[:].bitcast(I32), 0)
         nc.vector.memset(warm_in[:], 1.0)
@@ -82,7 +85,7 @@ def tile_picked_ytani_act_p_kernel(
         nc.sync.dma_start(out=qa_tab[ACT_ROW : ACT_ROW + 1, :], in_=act[0:1, :])
         nc.scalar.activation(warm_out[:], warm_in[:], ACT.Abs_reciprocal_sqrt)
 
-        xs_picked = keep.tile([P, S], U8, name="xs_picked", align_bytes=64)
+        xs_picked = tile("xs_picked", [P, S], U8)
         nc.vector.tensor_copy(xs_picked[:], xs_tab[:].indirect(offs_sb[:]))
         place_scale_rows(nc, xs, xs_picked)
         nc.sync.dma_start(out=ew_tab[:].bitcast(I32), in_=e_words[0].rearrange("p n t -> p (n t)").bitcast(I32))
@@ -90,7 +93,7 @@ def tile_picked_ytani_act_p_kernel(
         nc.vector.tensor_copy(es_picked[:, 0:V], es_tab[:].indirect(refs_sb[:]))
         place_scale_rows(nc, es, es_picked)
 
-        w_bf = keep.tile([P, PACK, P, PACK], BF16, name="w_bf", align_bytes=64)
+        w_bf = tile("w_bf", [P, PACK, P, PACK], BF16)
 
         def cast_w(copy, m0, m1):
             u, base = divmod(m0, P // 2)
@@ -100,36 +103,31 @@ def tile_picked_ytani_act_p_kernel(
             )
 
         cast_w(nc.scalar.copy, 0, 64)
-        cast_w(nc.scalar.copy, 64, 96)
-        cast_w(nc.vector.tensor_copy, 96, 128)
-        wq = keep.tile([P, H], U32, name="wq", align_bytes=64)
-        ws = keep.tile([P, H], U8, name="ws", align_bytes=64)
+        cast_w(nc.scalar.copy, 64, W_SCALAR_END)
+        cast_w(nc.vector.tensor_copy, W_SCALAR_END, P)
+        wq = tile("wq", [P, H], U32)
+        ws = tile("ws", [P, H], U8)
         nc.vector.quantize_mx(out=wq[:].bitcast(FP8X4), scales=ws[:], in_=w_bf[:].rearrange("p j m r -> p (j m r)"))
 
-        own_row = [keep.tile([P, HALF], F32, name="own_row%d" % u, align_bytes=64) for u in range(2)]
-
+        own_row = tile("own_row", [P, S], F32)
         own_ps = psum.tile([P, PACK, P], F32, name="own_ps", tag="s3")
         for c in range(PACK):
             nc.tensor.transpose(own_ps[:, c, :], own_col[:, c : c + 1].to_broadcast([P, P]), ident[:])
-        for u in range(2):
-            nc.scalar.activation(
-                own_row[u][:].rearrange("p (n c) -> p n c", c=PACK),
-                own_ps[:, :, u * 64 : (u + 1) * 64].rearrange("p c n -> p n c"),
-                ACT.Copy,
-                scale=1.0 / Y_SCALE,
-            )
+        nc.scalar.activation(
+            own_row[:].rearrange("p (n c) -> p n c", c=PACK), own_ps[:].rearrange("p c n -> p n c"), ACT.Copy, scale=1.0 / Y_SCALE
+        )
 
-        xq = [
-            keep.tile([P, HALF], U32, name="xq0", align_bytes=64),
-            keep.tile([P, HALF], U32, name="xq1", align_bytes=64),
-        ]
-        for u in range(2):
-            nc.vector.tensor_copy(xq[u][:], xw_tab[:].indirect(offs_sb[:, 16 * u : 16 * (u + 1)]))
+        x_cuts = ((0, P), (P, 2 * P), (2 * P, S))
+        xq = []
+        for i, (t0, t1) in enumerate(x_cuts):
+            piece = tile("xq%d" % i, [P, t1 - t0], U32)
+            nc.vector.tensor_copy(piece[:], xw_tab[:].indirect(offs_sb[:, t0 // 16 : t1 // 16]))
+            xq += [piece[:, t - t0 : t - t0 + P] for t in range(t0, t1, P)]
 
-        qa = keep.tile([P, V], F32, name="qa", align_bytes=64)
+        qa = tile("qa", [P, V], F32)
         nc.vector.tensor_copy(qa[:], qa_tab[:].indirect(refs_sb[:]))
-        hs = [keep.tile([P, HALF], U8, name="hs%d" % u, align_bytes=64) for u in range(2)]
-        h_bf = [keep.tile([P, HALF, PACK], BF16, name="h_bf%d" % u, align_bytes=64) for u in range(2)]
+
+        h_bf = [tile("h_bf0", [P, HALF, PACK], BF16), tile("h_bf1", [P, HALF, PACK], BF16)]
         for c in range(NB):
             h_ps = psum.tile([P, PACK, P], F32, name="h_ps%d" % c, tag="h%d" % c)
             cols = slice((c % 2) * P, (c % 2 + 1) * P)
@@ -138,7 +136,7 @@ def tile_picked_ytani_act_p_kernel(
                     out=h_ps[:, j, :],
                     lhsT=wq[:, j * P : (j + 1) * P].bitcast(FP8X4),
                     lhsT_scale=ws[:, j * P : (j + 1) * P],
-                    rhs=xq[c // 2][:, cols].bitcast(FP8X4),
+                    rhs=xq[c].bitcast(FP8X4),
                     rhs_scale=xs[:, c * P : (c + 1) * P],
                     start=True,
                     stop=True,
@@ -148,134 +146,113 @@ def tile_picked_ytani_act_p_kernel(
         qa_ps = psum.tile([P, NB, P], F32, name="qa_ps", tag="h1")
         for b in range(NB):
             nc.tensor.transpose(qa_ps[:, b, :], qa[:, b * P : (b + 1) * P], ident[:])
-        qa_col = keep.tile([P, NB, 2], F32, name="qa_col")
+        qn_own = {}
+        for (u, b), successor in (((1, 2), "num0"),):
+            qn_own[u, b] = tile("qn%d%d" % (u, b), [P, 1], F32, tag=successor)
+            nc.scalar.activation(qn_own[u, b][:], qa_ps[:, b, QN_ROW : QN_ROW + 1], ACT.Copy, scale=1.0 / Y_SCALE)
+        qa_col = tile("qa_col", [P, NB, 2], F32)
         nc.scalar.activation(qa_col[:], qa_ps[:, :, QN_ROW : ACT_ROW + 1 : ACT_ROW - QN_ROW], ACT.Copy, scale=1.0 / Y_SCALE)
 
+        hq, hs, eq, s_ps, sgn, num = {}, {}, {}, {}, {}, {}
+        dneg = [tile("dneg%d" % u, [P, NB, HALF], F32) for u in range(2)]
+        root = [tile("root%d" % u, [P, NB, HALF], F32) for u in range(2)]
+        inv = [tile("inv%d" % u, [P, NB, HALF], F32) for u in range(2)]
+
         def quantize_h(u):
+            hq[u] = late.tile([P, HALF], U32, name="hq%d" % u, offset=8 * HALF * u, align_bytes=64)
+            hs[u] = tile("hs%d" % u, [P, HALF], U8)
             nc.vector.quantize_mx(out=hq[u][:].bitcast(FP8X4), scales=hs[u][:], in_=h_bf[u][:].rearrange("p n j -> p (n j)"))
 
         def gather_e(g):
-            nc.vector.tensor_copy(eq[g][:], ew_tab[:].indirect(refs_sb[:, 16 * g : 16 * (g + 1)]))
+            pair = late.tile([P, HALF], U32, name="eq1", offset=4 * HALF, align_bytes=64) if g else tile("eq0", [P, HALF], U32)
+            nc.vector.tensor_copy(pair[:], ew_tab[:].indirect(refs_sb[:, 16 * g : 16 * (g + 1)]))
+            eq[2 * g], eq[2 * g + 1] = pair[:, 0:P], pair[:, P:HALF]
 
-        eq = [keep.tile([P, HALF], U32, name="eq0", align_bytes=64)]
+        def product(u, b):
+            if u == 0:
+                s_ps[b] = psum.tile([P, 2, HALF], F32, name="s_ps%d" % b, tag="s%d" % b)
+            nc.tensor.matmul_mx(
+                out=s_ps[b][:, u, :],
+                lhsT=eq[b].bitcast(FP8X4),
+                lhsT_scale=es[:, b * P : (b + 1) * P],
+                rhs=hq[u][:].bitcast(FP8X4),
+                rhs_scale=hs[u][:],
+                start=True,
+                stop=True,
+            )
+
+        def denominators(u, b):
+            qn_col = qn_own[u, b][:] if (u, b) in qn_own else qa_col[:, b, 0:1]
+            own_half = own_row[:, u * HALF : (u + 1) * HALF]
+            nc.vector.scalar_tensor_tensor(dneg[u][:, b, :], s_ps[b][:, u, :], qn_col, own_half, ALU.subtract, ALU.subtract)
+
+        def signs(u, b0, b1):
+            if u not in sgn:
+                sgn[u] = tile("sgn%d" % u, [P, NB, HALF], F32)
+            nc.gpsimd.tensor_scalar(sgn[u][:, b0:b1, :], dneg[u][:, b0:b1, :], TINY, -TINY, ALU.min, ALU.max)
+
+        def roots(u, b0, b1):
+            nc.scalar.activation(root[u][:, b0:b1, :], dneg[u][:, b0:b1, :], ACT.Abs_reciprocal_sqrt)
+
+        def squares(u, b0, b1, t0=0, t1=HALF):
+            nc.scalar.activation(inv[u][:, b0:b1, t0:t1], root[u][:, b0:b1, t0:t1], ACT.Square)
+
+        def numerators(u):
+            num[u] = tile("num%d" % u, [P, NB, HALF], F32)
+            for b in range(NB):
+                nc.vector.scalar_tensor_tensor(num[u][:, b, :], s_ps[b][:, u, :], qa_col[:, b, 1:2], sgn[u][:, b, :], ALU.mult, ALU.mult)
+
+        o_ps = {}
+
+        def quotients(c, b0, b1, bank):
+            u, cols = c // 2, slice((c % 2) * P, (c % 2 + 1) * P)
+            arg = tile("arg%d%d" % (c, b0), [P, b1 - b0, P], F32)
+            nc.vector.tensor_tensor(arg[:], num[u][:, b0:b1, cols], inv[u][:, b0:b1, cols], ALU.mult)
+            o_ps[c, b0] = psum.tile([P, (b1 - b0) * P], F32, name="o_ps%d%d" % (c, b0), tag=bank)
+            for b in range(b1 - b0):
+                nc.tensor.transpose(o_ps[c, b0][:, b * P : (b + 1) * P], arg[:, b, :], ident[:])
+
+        def finish(c, b0, b1, queue):
+            res = tile("res%d%d" % (c, b0), [P, (b1 - b0) * P], F32)
+            nc.scalar.activation(res[:], o_ps[c, b0][:], ACT.Tanh, scale=-Y_SCALE / TINY)
+            queue.dma_start(out=out[c * P : (c + 1) * P, b0 * P : b1 * P], in_=res[:])
+
         gather_e(0)
-        hq = [
-            late.tile([P, HALF], U32, name="hq0", offset=0, align_bytes=64),
-            late.tile([P, HALF], U32, name="hq1", offset=8 * HALF, align_bytes=64),
-        ]
-        eq.append(late.tile([P, HALF], U32, name="eq1", offset=4 * HALF, align_bytes=64))
         quantize_h(0)
         gather_e(1)
         quantize_h(1)
-
-        s_ps, dneg, root, sgn, num, inv, arg = {}, {}, {}, {}, {}, {}, {}
-        for u in range(2):
-            for g in range(2):
-                for group, label in ((dneg, "dneg"), (root, "root"), (sgn, "sgn"), (arg, "arg")):
-                    group[u, g] = keep.tile([P, 2, HALF], F32, name="%s%d%d" % (label, u, g), align_bytes=64)
-
-        def product(u, g):
-            if (u, g) == (0, 0):
-                sp = [psum.tile([P, HALF], F32, name="s_ps0_%d" % e, tag=bank)[:] for e, bank in enumerate(("h0", "s0"))]
-            else:
-                both = psum.tile([P, 2, HALF], F32, name="s_ps%d%d" % (u, g), tag="s%d" % (2 * u + g))
-                sp = [both[:, e, :] for e in range(2)]
-            for e in range(2):
-                b = 2 * g + e
-                nc.tensor.matmul_mx(
-                    out=sp[e],
-                    lhsT=eq[g][:, e * P : (e + 1) * P].bitcast(FP8X4),
-                    lhsT_scale=es[:, b * P : (b + 1) * P],
-                    rhs=hq[u][:].bitcast(FP8X4),
-                    rhs_scale=hs[u][:],
-                    start=True,
-                    stop=True,
-                )
-            s_ps[u, g] = sp
-
-        def denominators(u, g):
-            for e in range(2):
-                qn_col = qa_col[:, 2 * g + e, 0:1]
-                nc.vector.scalar_tensor_tensor(dneg[u, g][:, e, :], s_ps[u, g][e], qn_col, own_row[u][:], ALU.subtract, ALU.subtract)
-            nc.gpsimd.tensor_scalar(sgn[u, g][:], dneg[u, g][:], TINY, -TINY, ALU.min, ALU.max)
-
-        def roots(u, g, e0=0, e1=2):
-            nc.scalar.activation(root[u, g][:, e0:e1, :], dneg[u, g][:, e0:e1, :], ACT.Abs_reciprocal_sqrt)
-
-        def squares(u, g, step=2):
-            inv[u, g] = keep.tile([P, 2, HALF], F32, name="inv%d%d" % (u, g), align_bytes=64)
-            for e in range(0, 2, step):
-                nc.scalar.activation(inv[u, g][:, e : e + step, :], root[u, g][:, e : e + step, :], ACT.Square)
-
-        def numerators(u, g, tag=None, c0=0, c1=2):
-            name = "num%d%d" % (u, g)
-            if c0 == 0:
-                num[u, g] = keep.tile([P, 2, HALF], F32, name=name, tag=tag or name, align_bytes=64)
-            cols = slice(c0 * P, c1 * P)
-            for e in range(2):
-                nc.vector.scalar_tensor_tensor(
-                    num[u, g][:, e, cols], s_ps[u, g][e][:, cols], qa_col[:, 2 * g + e, 1:2], sgn[u, g][:, e, cols], ALU.mult, ALU.mult
-                )
-
-        def quotients(u, g, c0, c1, e0=0, e1=2):
-            cols = slice(c0 * P, c1 * P)
-            nc.vector.tensor_tensor(arg[u, g][:, e0:e1, cols], num[u, g][:, e0:e1, cols], inv[u, g][:, e0:e1, cols], ALU.mult)
-
-        def finish(u, g, c0, c1, bank, tag=None):
-            name = "%d%d%d" % (u, g, c0)
-            o_ps = psum.tile([P, c1 - c0, HALF], F32, name="o_ps" + name, tag=bank)
-            for c in range(c0, c1):
-                for e in range(2):
-                    nc.tensor.transpose(o_ps[:, c - c0, e * P : (e + 1) * P], arg[u, g][:, e, c * P : (c + 1) * P], ident[:])
-            res = keep.tile([P, c1 - c0, HALF], F32, name="res" + name, tag=tag or "res" + name, align_bytes=64)
-            for c in range(c0, c1):
-                nc.scalar.activation(res[:, c - c0, :], o_ps[:, c - c0, :], ACT.Tanh, scale=-Y_SCALE / TINY)
-                rows = slice(u * HALF + c * P, u * HALF + (c + 1) * P)
-                nc.sync.dma_start(out=out[rows, g * HALF : (g + 1) * HALF], in_=res[:, c - c0, :])
-
-        product(0, 0)
-        product(0, 1)
-        denominators(0, 0)
-        product(1, 0)
-        product(1, 1)
-        denominators(0, 1)
-        roots(0, 0, 0, 1)
-        roots(0, 0, 1, 2)
-        squares(0, 0, 1)
-        roots(0, 1)
-        squares(0, 1)
-        denominators(1, 0)
-        denominators(1, 1)
-        roots(1, 0)
-        roots(1, 1)
-        squares(1, 0)
-        inv[1, 1] = keep.tile([P, 2, HALF], F32, name="inv11", align_bytes=64)
-        nc.scalar.activation(inv[1, 1][:, :, 0:SQ_SCALAR], root[1, 1][:, :, 0:SQ_SCALAR], ACT.Square)
-        tanh_warm = keep.tile([P, 1], F32, name="tanh_warm")
-        nc.scalar.activation(tanh_warm[:], root[1, 1][:, 1, 0:1], ACT.Tanh)
-        numerators(0, 0, "own_row1")
-        numerators(0, 1, "num01")
-        quotients(0, 0, 0, 2)
-        finish(0, 0, 0, 1, "h1", "dneg11")
-        finish(0, 0, 1, 2, "h2")
-        quotients(0, 1, 0, 2)
-        finish(0, 1, 0, 1, "h3")
-        finish(0, 1, 1, 2, "h0")
-        numerators(1, 0)
-        nc.vector.tensor_tensor(inv[1, 1][:, :, SQ_SCALAR:], root[1, 1][:, :, SQ_SCALAR:], root[1, 1][:, :, SQ_SCALAR:], ALU.mult)
-        numerators(1, 1, None, 0, 1)
-        quotients(1, 0, 0, 1)
-        finish(1, 0, 0, 1, "s0")
-        quotients(1, 0, 1, 2)
-        finish(1, 0, 1, 2, "s1")
-        quotients(1, 1, 0, 1)
-        finish(1, 1, 0, 1, "s2")
-        numerators(1, 1, None, 1, 2)
-        quotients(1, 1, 1, 2, 0, 1)
-        quotients(1, 1, 1, 2, 1, 2)
-        last = keep.tile([P, HALF], F32, name="res_last", align_bytes=64)
-        for e, bank in enumerate(("h1", "h2")):
-            o_ps = psum.tile([P, P], F32, name="o_ps_last%d" % e, tag=bank)
-            nc.tensor.transpose(o_ps[:], arg[1, 1][:, e, P:HALF], ident[:])
-            nc.scalar.activation(last[:, e * P : (e + 1) * P], o_ps[:], ACT.Tanh, scale=-Y_SCALE / TINY)
-        nc.scalar.dma_start(out=out[HALF + P : S, HALF:V], in_=last[:])
+        for b in range(NB):
+            product(0, b)
+        for b in range(NB):
+            denominators(0, b)
+            product(1, b)
+            if b < 2:
+                roots(0, b, b + 1)
+            if b % 2:
+                signs(0, b - 1, b + 1)
+        roots(0, 2, NB)
+        for b in range(NB):
+            denominators(1, b)
+            if b % 2:
+                roots(1, b - 1, b + 1)
+                signs(1, b - 1, b + 1)
+        squares(0, 0, NB, 0, P)
+        squares(0, 0, NB, P, HALF)
+        tanh_warm = tile("tanh_warm", [P, 1], F32)
+        nc.scalar.activation(tanh_warm[:], root[1][:, NB - 1, 0:1], ACT.Tanh)
+        numerators(0)
+        quotients(0, 0, NB, "h0")
+        finish(0, 0, NB, nc.sync)
+        quotients(1, 0, NB, "h1")
+        nc.vector.tensor_tensor(inv[1][:, :, 0:P], root[1][:, :, 0:P], root[1][:, :, 0:P], ALU.mult)
+        squares(1, 0, NB, P, HALF)
+        finish(1, 0, NB, nc.sync)
+        numerators(1)
+        quotients(2, 0, 2, "h2")
+        finish(2, 0, 2, nc.sync)
+        quotients(2, 2, NB, "h3")
+        finish(2, 2, NB, nc.sync)
+        quotients(3, 0, 2, "s0")
+        finish(3, 0, 2, nc.sync)
+        quotients(3, 2, NB, "s1")
+        finish(3, 2, NB, nc.scalar)

@@ -156,7 +156,7 @@ def tile_picked_ytani_act_p_kernel(
         hq, hs, eq, s_ps, sgn, num = {}, {}, {}, {}, {}, {}
         dneg = [tile("dneg%d" % u, [P, NB, HALF], F32) for u in range(2)]
         root = [tile("root%d" % u, [P, NB, HALF], F32) for u in range(2)]
-        inv = [tile("inv%d" % u, [P, NB, HALF], F32) for u in range(2)]
+        inv = {}
 
         def quantize_h(u):
             hq[u] = late.tile([P, HALF], U32, name="hq%d" % u, offset=8 * HALF * u, align_bytes=64)
@@ -194,23 +194,34 @@ def tile_picked_ytani_act_p_kernel(
         def roots(u, b0, b1):
             nc.scalar.activation(root[u][:, b0:b1, :], dneg[u][:, b0:b1, :], ACT.Abs_reciprocal_sqrt)
 
-        def squares(u, b0, b1, t0=0, t1=HALF):
-            nc.scalar.activation(inv[u][:, b0:b1, t0:t1], root[u][:, b0:b1, t0:t1], ACT.Square)
+        def roots_of(c, b0, b1):
+            return root[c // 2][:, b0:b1, (c % 2) * P : (c % 2 + 1) * P]
 
-        def numerators(u):
-            num[u] = tile("num%d" % u, [P, NB, HALF], F32)
-            for b in range(NB):
+        def squares(c, b0=0, b1=NB, on_vector=False):
+            if b0 == 0:
+                inv[c] = tile("inv%d" % c, [P, NB, P], F32)
+            if on_vector:
+                nc.vector.tensor_tensor(inv[c][:, b0:b1, :], roots_of(c, b0, b1), roots_of(c, b0, b1), ALU.mult)
+            else:
+                nc.scalar.activation(inv[c][:, b0:b1, :], roots_of(c, b0, b1), ACT.Square)
+
+        def numerators(u, b0, b1):
+            if b0 == 0:
+                num[u] = tile("num%d" % u, [P, NB, HALF], F32)
+            for b in range(b0, b1):
                 nc.vector.scalar_tensor_tensor(num[u][:, b, :], s_ps[b][:, u, :], qa_col[:, b, 1:2], sgn[u][:, b, :], ALU.mult, ALU.mult)
 
         o_ps = {}
 
-        def quotients(c, b0, b1, bank):
+        def quotients(c, cuts, bank):
             u, cols = c // 2, slice((c % 2) * P, (c % 2 + 1) * P)
-            arg = tile("arg%d%d" % (c, b0), [P, b1 - b0, P], F32)
-            nc.vector.tensor_tensor(arg[:], num[u][:, b0:b1, cols], inv[u][:, b0:b1, cols], ALU.mult)
-            o_ps[c, b0] = psum.tile([P, (b1 - b0) * P], F32, name="o_ps%d%d" % (c, b0), tag=bank)
-            for b in range(b1 - b0):
-                nc.tensor.transpose(o_ps[c, b0][:, b * P : (b + 1) * P], arg[:, b, :], ident[:])
+            first = cuts[0]
+            o_ps[c, first] = psum.tile([P, (cuts[-1] - first) * P], F32, name="o_ps%d%d" % (c, first), tag=bank)
+            for b0, b1 in zip(cuts, cuts[1:]):
+                arg = tile("arg%d%d" % (c, b0), [P, b1 - b0, P], F32)
+                nc.vector.tensor_tensor(arg[:], num[u][:, b0:b1, cols], inv[c][:, b0:b1, :], ALU.mult)
+                for b in range(b0, b1):
+                    nc.tensor.transpose(o_ps[c, first][:, (b - first) * P : (b - first + 1) * P], arg[:, b - b0, :], ident[:])
 
         def finish(c, b0, b1, queue):
             res = tile("res%d%d" % (c, b0), [P, (b1 - b0) * P], F32)
@@ -230,29 +241,34 @@ def tile_picked_ytani_act_p_kernel(
                 roots(0, b, b + 1)
             if b % 2:
                 signs(0, b - 1, b + 1)
+            if b == 1:
+                squares(0, 0, 2)
         roots(0, 2, NB)
         for b in range(NB):
             denominators(1, b)
             if b % 2:
                 roots(1, b - 1, b + 1)
                 signs(1, b - 1, b + 1)
-        squares(0, 0, NB, 0, P)
-        squares(0, 0, NB, P, HALF)
+            if b == 1:
+                squares(0, 2, NB)
+        squares(1)
         tanh_warm = tile("tanh_warm", [P, 1], F32)
         nc.scalar.activation(tanh_warm[:], root[1][:, NB - 1, 0:1], ACT.Tanh)
-        numerators(0)
-        quotients(0, 0, NB, "h0")
+        squares(3)
+        numerators(0, 0, NB)
+        numerators(1, 0, 1)
+        quotients(0, (0, NB), "h0")
         finish(0, 0, NB, nc.sync)
-        quotients(1, 0, NB, "h1")
-        nc.vector.tensor_tensor(inv[1][:, :, 0:P], root[1][:, :, 0:P], root[1][:, :, 0:P], ALU.mult)
-        squares(1, 0, NB, P, HALF)
+        quotients(1, (0, NB), "h1")
+        numerators(1, 1, 3)
+        squares(2, on_vector=True)
         finish(1, 0, NB, nc.sync)
-        numerators(1)
-        quotients(2, 0, 2, "h2")
+        numerators(1, 3, NB)
+        quotients(2, (0, 2), "h2")
         finish(2, 0, 2, nc.sync)
-        quotients(2, 2, NB, "h3")
+        quotients(2, (2, NB), "h3")
         finish(2, 2, NB, nc.sync)
-        quotients(3, 0, 2, "s0")
+        quotients(3, (0, 2), "s0")
         finish(3, 0, 2, nc.sync)
-        quotients(3, 2, NB, "s1")
+        quotients(3, (2, NB), "s1")
         finish(3, 2, NB, nc.scalar)

@@ -237,30 +237,26 @@ def tile_picked_ytani_act_p_kernel(
         for b in range(NB):
             denominators(0, b)
             product(1, b)
-            if b < 2:
-                roots(0, b, b + 1)
+            roots(0, b, b + 1)
             if b % 2:
                 signs(0, b - 1, b + 1)
-            if b == 1:
-                squares(0, 0, 2)
-        roots(0, 2, NB)
         for b in range(NB):
             denominators(1, b)
             if b % 2:
-                roots(1, b - 1, b + 1)
                 signs(1, b - 1, b + 1)
-            if b == 1:
-                squares(0, 2, NB)
+        roots(1, 0, 1)
+        squares(0)
+        roots(1, 1, NB)
         squares(1)
         tanh_warm = tile("tanh_warm", [P, 1], F32)
         nc.scalar.activation(tanh_warm[:], root[1][:, NB - 1, 0:1], ACT.Tanh)
         squares(3)
         numerators(0, 0, NB)
-        numerators(1, 0, 1)
+        numerators(1, 0, 2)
         quotients(0, (0, NB), "h0")
         finish(0, 0, NB, nc.sync)
         quotients(1, (0, NB), "h1")
-        numerators(1, 1, 3)
+        numerators(1, 2, 3)
         squares(2, on_vector=True)
         finish(1, 0, NB, nc.sync)
         numerators(1, 3, NB)

@@ -153,8 +153,11 @@ def tile_picked_ytani_act_p_kernel(
         qa_col = tile("qa_col", [P, NB, 2], F32)
         nc.scalar.activation(qa_col[:], qa_ps[:, :, QN_ROW : ACT_ROW + 1 : ACT_ROW - QN_ROW], ACT.Copy, scale=1.0 / Y_SCALE)
 
-        hq, hs, eq, s_ps, sgn, num = {}, {}, {}, {}, {}, {}
-        dneg = [tile("dneg%d" % u, [P, NB, HALF], F32) for u in range(2)]
+        hq, hs, eq, s_ps, num = {}, {}, {}, {}, {}
+        dneg_all = tile("dneg", [P, 2 * NB, HALF], F32)
+        sgn_all = tile("sgn", [P, 2 * NB, HALF], F32)
+        dneg = [dneg_all[:, u * NB : (u + 1) * NB, :] for u in range(2)]
+        sgn = [sgn_all[:, u * NB : (u + 1) * NB, :] for u in range(2)]
         root = [tile("root%d" % u, [P, NB, HALF], F32) for u in range(2)]
         inv = {}
 
@@ -186,10 +189,8 @@ def tile_picked_ytani_act_p_kernel(
             own_half = own_row[:, u * HALF : (u + 1) * HALF]
             nc.vector.scalar_tensor_tensor(dneg[u][:, b, :], s_ps[b][:, u, :], qn_col, own_half, ALU.subtract, ALU.subtract)
 
-        def signs(u, b0, b1):
-            if u not in sgn:
-                sgn[u] = tile("sgn%d" % u, [P, NB, HALF], F32)
-            nc.gpsimd.tensor_scalar(sgn[u][:, b0:b1, :], dneg[u][:, b0:b1, :], TINY, -TINY, ALU.min, ALU.max)
+        def signs(i0, i1):
+            nc.gpsimd.tensor_scalar(sgn_all[:, i0:i1, :], dneg_all[:, i0:i1, :], TINY, -TINY, ALU.min, ALU.max)
 
         def roots(u, b0, b1):
             nc.scalar.activation(root[u][:, b0:b1, :], dneg[u][:, b0:b1, :], ACT.Abs_reciprocal_sqrt)
@@ -238,12 +239,10 @@ def tile_picked_ytani_act_p_kernel(
             denominators(0, b)
             product(1, b)
             roots(0, b, b + 1)
-            if b % 2:
-                signs(0, b - 1, b + 1)
         for b in range(NB):
             denominators(1, b)
-            if b % 2:
-                signs(1, b - 1, b + 1)
+        for i0, i1 in ((0, 1), (1, 3), (3, 6), (6, 8)):
+            signs(i0, i1)
         roots(1, 0, 1)
         squares(0)
         roots(1, 1, NB)

@@ -23,9 +23,10 @@ NB = 4
 HALF = 256
 Y_SCALE = 0.3
 TINY = 2.0**-60
-QN_ROW = 0
-ACT_ROW = 64
-W_SCALAR_END = 96
+QN_ROW = 4
+ACT_ROW = 68
+CLEAR_SPLIT = 1536
+W_SCALAR_END = 64
 
 
 def load_scale_rows(nc, table, rows):
@@ -56,7 +57,7 @@ def tile_picked_ytani_act_p_kernel(
         qa_tab = tile("qa_tab", [P, W], F32)
         xw_tab = tile("xw_tab", [P, T], U32)
         ew_tab = tile("ew_tab", [P, W], U32)
-        w_raw = [tile("w_raw%d" % u, [P, PACK, HALF], F32) for u in range(2)]
+        w_raw = tile("w_raw", [P, PACK, H], F32)
         own_col = tile("own_col", [P, PACK], F32)
         ident = tile("ident", [P, P], F32)
         warm_in = tile("warm_in", [P, 1], F32)
@@ -64,30 +65,31 @@ def tile_picked_ytani_act_p_kernel(
         xs = tile("xs", [P, S], U8)
         es = tile("es", [P, V], U8)
 
-        nc.vector.memset(xs_tab[:].bitcast(I32), 0)
+        nc.gpsimd.memset(xs_tab[:].bitcast(I32), 0)
+        nc.vector.memset(warm_in[:], 0.0)
         nc.vector.memset(es_tab[:].bitcast(I32), 0)
-        nc.vector.memset(warm_in[:], 1.0)
-        nc.vector.memset(qa_tab[:], 0.0)
-        make_identity(nc, ident[:])
         nc.vector.memset(xs[:].bitcast(I32), 0)
         nc.vector.memset(es[:].bitcast(I32), 0)
+        nc.vector.memset(qa_tab[:, 0:CLEAR_SPLIT], 0.0)
+        make_identity(nc, ident[:])
+        nc.scalar.activation(warm_out[:], warm_in[:], ACT.Abs_reciprocal_sqrt, bias=1.0)
+        nc.scalar.copy(out=qa_tab[:, CLEAR_SPLIT:W], in_=warm_in[:].to_broadcast([P, W - CLEAR_SPLIT]))
 
         w_rows = w1.rearrange("(p r) c -> p r c", r=PACK)
-        nc.sync.dma_start(out=w_raw[0][:], in_=w_rows[:, :, 0:HALF])
+        nc.sync.dma_start(out=w_raw[:, 0, :], in_=w_rows[:, 0, :])
         nc.sync.dma_start(offs_sb[:], offs)
         nc.sync.dma_start(refs_sb[:], refs)
         load_scale_rows(nc, xs_tab, x_scales)
-        nc.sync.dma_start(out=w_raw[1][:], in_=w_rows[:, :, HALF : 2 * HALF])
         load_scale_rows(nc, es_tab, e_scales)
         nc.sync.dma_start(out=own_col[:], in_=own.rearrange("(p c) o -> p (c o)", c=PACK))
+        nc.sync.dma_start(out=w_raw[:, 1:PACK, :], in_=w_rows[:, 1:PACK, :])
         nc.sync.dma_start(out=xw_tab[:].bitcast(I32), in_=x_words[0].rearrange("p n t -> p (n t)").bitcast(I32))
-        nc.sync.dma_start(out=qa_tab[QN_ROW : QN_ROW + 1, :], in_=qn[0:1, :])
-        nc.sync.dma_start(out=qa_tab[ACT_ROW : ACT_ROW + 1, :], in_=act[0:1, :])
-        nc.scalar.activation(warm_out[:], warm_in[:], ACT.Abs_reciprocal_sqrt)
 
         xs_picked = tile("xs_picked", [P, S], U8)
         nc.vector.tensor_copy(xs_picked[:], xs_tab[:].indirect(offs_sb[:]))
         place_scale_rows(nc, xs, xs_picked)
+        nc.sync.dma_start(out=qa_tab[QN_ROW : QN_ROW + 1, :], in_=qn[0:1, :])
+        nc.sync.dma_start(out=qa_tab[ACT_ROW : ACT_ROW + 1, :], in_=act[0:1, :])
         nc.sync.dma_start(out=ew_tab[:].bitcast(I32), in_=e_words[0].rearrange("p n t -> p (n t)").bitcast(I32))
         es_picked = late.tile([P, 4 * HALF + 128], U8, name="es_picked", offset=4 * HALF - 64, align_bytes=64)
         nc.vector.tensor_copy(es_picked[:, 0:V], es_tab[:].indirect(refs_sb[:]))
@@ -95,16 +97,11 @@ def tile_picked_ytani_act_p_kernel(
 
         w_bf = tile("w_bf", [P, PACK, P, PACK], BF16)
 
-        def cast_w(copy, m0, m1):
-            u, base = divmod(m0, P // 2)
+        for copy, m0, m1 in ((nc.scalar.copy, 0, W_SCALAR_END), (nc.vector.tensor_copy, W_SCALAR_END, P)):
             copy(
                 out=w_bf[:, :, m0:m1, :].rearrange("p j m r -> p m j r"),
-                in_=w_raw[u][:, :, PACK * base : PACK * (base + m1 - m0)].rearrange("p r (m j) -> p m j r", j=PACK),
+                in_=w_raw[:, :, PACK * m0 : PACK * m1].rearrange("p r (m j) -> p m j r", j=PACK),
             )
-
-        cast_w(nc.scalar.copy, 0, 64)
-        cast_w(nc.scalar.copy, 64, W_SCALAR_END)
-        cast_w(nc.vector.tensor_copy, W_SCALAR_END, P)
         wq = tile("wq", [P, H], U32)
         ws = tile("ws", [P, H], U8)
         nc.vector.quantize_mx(out=wq[:].bitcast(FP8X4), scales=ws[:], in_=w_bf[:].rearrange("p j m r -> p (j m r)"))

@@ -54,7 +54,7 @@ def tile_picked_ytani_act_p_kernel(
         refs_sb = keep.tile([P, V // 16], U16, name="refs_sb")
         xs_tab = tile("xs_tab", [P, T], U8)
         es_tab = tile("es_tab", [P, W], U8)
-        qa_tab = tile("qa_tab", [P, W], F32)
+        qa_tab = late.tile([P, W], F32, name="qa_tab", offset=8192, align_bytes=64)
         xw_tab = tile("xw_tab", [P, T], U32)
         ew_tab = tile("ew_tab", [P, W], U32)
         w_raw = tile("w_raw", [P, PACK, H], F32)
@@ -122,12 +122,13 @@ def tile_picked_ytani_act_p_kernel(
             xq += [piece[:, t - t0 : t - t0 + P] for t in range(t0, t1, P)]
 
         qa = tile("qa", [P, V], F32)
-        nc.vector.tensor_copy(qa[:], qa_tab[:].indirect(refs_sb[:]))
+        nc.scalar.activation(qa[:], qa_tab[:].indirect(refs_sb[:]), ACT.Copy)
 
-        h_bf = [tile("h_bf0", [P, HALF, PACK], BF16), tile("h_bf1", [P, HALF, PACK], BF16)]
+        h_first = [tile("h_bf0a", [P, P, PACK], BF16), late.tile([P, P, PACK], BF16, name="h_bf0b", offset=8192, align_bytes=64)]
+        h_second = late.tile([P, HALF, PACK], BF16, name="h_bf1", offset=8192 + 1024, align_bytes=64)
+        h_bf = [h_first[0][:], h_first[1][:], h_second[:, 0:P, :], h_second[:, P:HALF, :]]
         for c in range(NB):
             h_ps = psum.tile([P, PACK, P], F32, name="h_ps%d" % c, tag="h%d" % c)
-            cols = slice((c % 2) * P, (c % 2 + 1) * P)
             for j in range(PACK):
                 nc.tensor.matmul_mx(
                     out=h_ps[:, j, :],
@@ -138,7 +139,7 @@ def tile_picked_ytani_act_p_kernel(
                     start=True,
                     stop=True,
                 )
-            nc.scalar.copy(out=h_bf[c // 2][:, cols, :], in_=h_ps[:].rearrange("p j n -> p n j"))
+            (nc.vector.tensor_copy if c == 0 else nc.scalar.copy)(out=h_bf[c], in_=h_ps[:].rearrange("p j n -> p n j"))
 
         qa_ps = psum.tile([P, NB, P], F32, name="qa_ps", tag="h1")
         for b in range(NB):
@@ -158,10 +159,10 @@ def tile_picked_ytani_act_p_kernel(
         root = [tile("root%d" % u, [P, NB, HALF], F32) for u in range(2)]
         inv = {}
 
-        def quantize_h(u):
-            hq[u] = late.tile([P, HALF], U32, name="hq%d" % u, offset=8 * HALF * u, align_bytes=64)
-            hs[u] = tile("hs%d" % u, [P, HALF], U8)
-            nc.vector.quantize_mx(out=hq[u][:].bitcast(FP8X4), scales=hs[u][:], in_=h_bf[u][:].rearrange("p n j -> p (n j)"))
+        def quantize_h(t0, values, words):
+            hq[t0] = words
+            hs[t0] = tile("hs%d" % t0, [P, values.shape[1]], U8)
+            nc.vector.quantize_mx(out=words[:].bitcast(FP8X4), scales=hs[t0][:], in_=values.rearrange("p n j -> p (n j)"))
 
         def gather_e(g):
             pair = late.tile([P, HALF], U32, name="eq1", offset=4 * HALF, align_bytes=64) if g else tile("eq0", [P, HALF], U32)
@@ -171,15 +172,16 @@ def tile_picked_ytani_act_p_kernel(
         def product(u, b):
             if u == 0:
                 s_ps[b] = psum.tile([P, 2, HALF], F32, name="s_ps%d" % b, tag="s%d" % b)
-            nc.tensor.matmul_mx(
-                out=s_ps[b][:, u, :],
-                lhsT=eq[b].bitcast(FP8X4),
-                lhsT_scale=es[:, b * P : (b + 1) * P],
-                rhs=hq[u][:].bitcast(FP8X4),
-                rhs_scale=hs[u][:],
-                start=True,
-                stop=True,
-            )
+            for t0, t1 in (((0, P), (P, HALF)), ((HALF, S),))[u]:
+                nc.tensor.matmul_mx(
+                    out=s_ps[b][:, u, t0 - u * HALF : t1 - u * HALF],
+                    lhsT=eq[b].bitcast(FP8X4),
+                    lhsT_scale=es[:, b * P : (b + 1) * P],
+                    rhs=hq[t0][:].bitcast(FP8X4),
+                    rhs_scale=hs[t0][:],
+                    start=True,
+                    stop=True,
+                )
 
         def denominators(u, b):
             qn_col = qn_own[u, b][:] if (u, b) in qn_own else qa_col[:, b, 0:1]
@@ -226,10 +228,11 @@ def tile_picked_ytani_act_p_kernel(
             nc.scalar.activation(res[:], o_ps[c, b0][:], ACT.Tanh, scale=-Y_SCALE / TINY)
             queue.dma_start(out=out[c * P : (c + 1) * P, b0 * P : b1 * P], in_=res[:])
 
+        quantize_h(0, h_bf[0], tile("hq0a", [P, P], U32))
         gather_e(0)
-        quantize_h(0)
+        quantize_h(P, h_bf[1], late.tile([P, P], U32, name="hq0b", offset=4 * P, align_bytes=64))
         gather_e(1)
-        quantize_h(1)
+        quantize_h(HALF, h_second[:], late.tile([P, HALF], U32, name="hq1", offset=8 * HALF, align_bytes=64))
         for b in range(NB):
             product(0, b)
         for b in range(NB):

@@ -24,9 +24,10 @@ HALF = 256
 Y_SCALE = 0.3
 TINY = 2.0**-60
 QN_ROW = 4
-ACT_ROW = 68
+ACT_ROW = 40
 CLEAR_SPLIT = 1536
-W_SCALAR_END = 64
+W_SCALAR_END = 92
+W_FIRST = 40
 
 
 def load_scale_rows(nc, table, rows):
@@ -57,7 +58,8 @@ def tile_picked_ytani_act_p_kernel(
         qa_tab = late.tile([P, W], F32, name="qa_tab", offset=8192, align_bytes=64)
         xw_tab = tile("xw_tab", [P, T], U32)
         ew_tab = tile("ew_tab", [P, W], U32)
-        w_raw = tile("w_raw", [P, PACK, H], F32)
+        w_cuts = (0, W_FIRST, P)
+        w_raw = [tile("w_raw%d" % u, [P, PACK, PACK * (w_cuts[u + 1] - w_cuts[u])], F32) for u in range(2)]
         own_col = tile("own_col", [P, PACK], F32)
         ident = tile("ident", [P, P], F32)
         warm_in = tile("warm_in", [P, 1], F32)
@@ -66,8 +68,8 @@ def tile_picked_ytani_act_p_kernel(
         es = tile("es", [P, V], U8)
 
         nc.gpsimd.memset(xs_tab[:].bitcast(I32), 0)
-        nc.vector.memset(warm_in[:], 0.0)
         nc.vector.memset(es_tab[:].bitcast(I32), 0)
+        nc.vector.memset(warm_in[:], 0.0)
         nc.vector.memset(xs[:].bitcast(I32), 0)
         nc.vector.memset(es[:].bitcast(I32), 0)
         nc.vector.memset(qa_tab[:, 0:CLEAR_SPLIT], 0.0)
@@ -76,13 +78,13 @@ def tile_picked_ytani_act_p_kernel(
         nc.scalar.copy(out=qa_tab[:, CLEAR_SPLIT:W], in_=warm_in[:].to_broadcast([P, W - CLEAR_SPLIT]))
 
         w_rows = w1.rearrange("(p r) c -> p r c", r=PACK)
-        nc.sync.dma_start(out=w_raw[:, 0, :], in_=w_rows[:, 0, :])
+        nc.sync.dma_start(out=w_raw[0][:], in_=w_rows[:, :, 0 : PACK * W_FIRST])
         nc.sync.dma_start(offs_sb[:], offs)
         nc.sync.dma_start(refs_sb[:], refs)
         load_scale_rows(nc, xs_tab, x_scales)
-        load_scale_rows(nc, es_tab, e_scales)
         nc.sync.dma_start(out=own_col[:], in_=own.rearrange("(p c) o -> p (c o)", c=PACK))
-        nc.sync.dma_start(out=w_raw[:, 1:PACK, :], in_=w_rows[:, 1:PACK, :])
+        load_scale_rows(nc, es_tab, e_scales)
+        nc.sync.dma_start(out=w_raw[1][:], in_=w_rows[:, :, PACK * W_FIRST : H])
         nc.sync.dma_start(out=xw_tab[:].bitcast(I32), in_=x_words[0].rearrange("p n t -> p (n t)").bitcast(I32))
 
         xs_picked = tile("xs_picked", [P, S], U8)
@@ -97,10 +99,10 @@ def tile_picked_ytani_act_p_kernel(
 
         w_bf = tile("w_bf", [P, PACK, P, PACK], BF16)
 
-        for copy, m0, m1 in ((nc.scalar.copy, 0, W_SCALAR_END), (nc.vector.tensor_copy, W_SCALAR_END, P)):
+        for copy, u, m0, m1 in ((nc.scalar.copy, 0, 0, W_FIRST), (nc.scalar.copy, 1, W_FIRST, W_SCALAR_END), (nc.vector.tensor_copy, 1, W_SCALAR_END, P)):
             copy(
                 out=w_bf[:, :, m0:m1, :].rearrange("p j m r -> p m j r"),
-                in_=w_raw[:, :, PACK * m0 : PACK * m1].rearrange("p r (m j) -> p m j r", j=PACK),
+                in_=w_raw[u][:, :, PACK * (m0 - w_cuts[u]) : PACK * (m1 - w_cuts[u])].rearrange("p r (m j) -> p m j r", j=PACK),
             )
         wq = tile("wq", [P, H], U32)
         ws = tile("ws", [P, H], U8)
@@ -121,8 +123,9 @@ def tile_picked_ytani_act_p_kernel(
             nc.vector.tensor_copy(piece[:], xw_tab[:].indirect(offs_sb[:, t0 // 16 : t1 // 16]))
             xq += [piece[:, t - t0 : t - t0 + P] for t in range(t0, t1, P)]
 
-        qa = tile("qa", [P, V], F32)
-        nc.scalar.activation(qa[:], qa_tab[:].indirect(refs_sb[:]), ACT.Copy)
+        qa = [tile("qa%d" % g, [P, HALF], F32) for g in range(2)]
+        for g in range(2):
+            nc.scalar.activation(qa[g][:], qa_tab[:].indirect(refs_sb[:, 16 * g : 16 * (g + 1)]), ACT.Copy)
 
         h_first = [tile("h_bf0a", [P, P, PACK], BF16), late.tile([P, P, PACK], BF16, name="h_bf0b", offset=8192, align_bytes=64)]
         h_second = late.tile([P, HALF, PACK], BF16, name="h_bf1", offset=8192 + 1024, align_bytes=64)
@@ -141,15 +144,21 @@ def tile_picked_ytani_act_p_kernel(
                 )
             (nc.vector.tensor_copy if c == 0 else nc.scalar.copy)(out=h_bf[c], in_=h_ps[:].rearrange("p j n -> p n j"))
 
-        qa_ps = psum.tile([P, NB, P], F32, name="qa_ps", tag="h1")
-        for b in range(NB):
-            nc.tensor.transpose(qa_ps[:, b, :], qa[:, b * P : (b + 1) * P], ident[:])
+        nc.vector.tensor_copy(out=qa[0][P // 2 : P, :], in_=qa[1][0 : P // 2, :])
+        qa_ps = psum.tile([P, 2, 2, P // 2], F32, name="qa_ps", tag="s2")
+        for i in range(2):
+            nc.tensor.transpose(qa_ps[:, i, :, :].rearrange("p g r -> p (g r)"), qa[0][:, i * P : (i + 1) * P], ident[:])
+        qa_col = tile("qa_col", [P, NB, 2], F32)
+        nc.scalar.activation(
+            qa_col[:].rearrange("p (g i) r -> p i g r", g=2),
+            qa_ps[:, :, :, QN_ROW : ACT_ROW + 1 : ACT_ROW - QN_ROW],
+            ACT.Copy,
+            scale=1.0 / Y_SCALE,
+        )
         qn_own = {}
         for (u, b), successor in (((1, 2), "num0"),):
             qn_own[u, b] = tile("qn%d%d" % (u, b), [P, 1], F32, tag=successor)
-            nc.scalar.activation(qn_own[u, b][:], qa_ps[:, b, QN_ROW : QN_ROW + 1], ACT.Copy, scale=1.0 / Y_SCALE)
-        qa_col = tile("qa_col", [P, NB, 2], F32)
-        nc.scalar.activation(qa_col[:], qa_ps[:, :, QN_ROW : ACT_ROW + 1 : ACT_ROW - QN_ROW], ACT.Copy, scale=1.0 / Y_SCALE)
+            nc.scalar.activation(qn_own[u, b][:], qa_ps[:, b % 2, b // 2, QN_ROW : QN_ROW + 1], ACT.Copy, scale=1.0 / Y_SCALE)
 
         hq, hs, eq, s_ps, num = {}, {}, {}, {}, {}
         dneg_all = tile("dneg", [P, 2 * NB, HALF], F32)
@@ -228,11 +237,15 @@ def tile_picked_ytani_act_p_kernel(
             nc.scalar.activation(res[:], o_ps[c, b0][:], ACT.Tanh, scale=-Y_SCALE / TINY)
             queue.dma_start(out=out[c * P : (c + 1) * P, b0 * P : b1 * P], in_=res[:])
 
-        quantize_h(0, h_bf[0], tile("hq0a", [P, P], U32))
+        quantize_h(0, h_bf[0], late.tile([P, P], U32, name="hq0a", offset=8192 + 3072, align_bytes=64))
         gather_e(0)
         quantize_h(P, h_bf[1], late.tile([P, P], U32, name="hq0b", offset=4 * P, align_bytes=64))
         gather_e(1)
-        quantize_h(HALF, h_second[:], late.tile([P, HALF], U32, name="hq1", offset=8 * HALF, align_bytes=64))
+        hq[HALF] = late.tile([P, HALF], U32, name="hq1", offset=8 * HALF, align_bytes=64)
+        hs[HALF] = tile("hs1", [P, HALF], U8)
+        for i in range(2):
+            cols = slice(i * P, (i + 1) * P)
+            nc.vector.quantize_mx(out=hq[HALF][:, cols].bitcast(FP8X4), scales=hs[HALF][:, cols], in_=h_bf[2 + i].rearrange("p n j -> p (n j)"))
         for b in range(NB):
             product(0, b)
         for b in range(NB):

from contextlib import ExitStack

import concourse.mybir as mybir
from concourse.masks import make_identity

K, T, S, H, V, W = 512, 2048, 512, 512, 512, 2048
FLOPS = 2 * K * H * S + 2 * H * S * V
BYTES = K * T + K * T // 32 + H * W + H * W // 32 + 4 * K * H + 2 * 4 * W + 4 * S + 2 * 2 * 128 * 32 + 4 * S * V

F32 = mybir.dt.float32
BF16 = mybir.dt.bfloat16
I32 = mybir.dt.int32
U32 = mybir.dt.uint32
U16 = mybir.dt.uint16
U8 = mybir.dt.uint8
FP8X4 = mybir.dt.float8_e4m3fn_x4
ACT = mybir.ActivationFunctionType
ALU = mybir.AluOpType

P = 128
PACK = 4
NB = 4
HALF = 256
Y_SCALE = 0.3
TINY = 2.0**-60
QN_ROW = 4
ACT_ROW = 40
CLEAR_SPLIT = 1536
W_SCALAR_END = 92
W_FIRST = 40


def load_scale_rows(nc, table, rows):
    nc.sync.dma_start(out=table[0:P:8, :].bitcast(I32), in_=rows[0].bitcast(I32))


def place_scale_rows(nc, plane, picked):
    for r in range(4):
        nc.sync.dma_start(out=plane[r:P:32, :].bitcast(I32), in_=picked[8 * r : P : 32, 0:V].bitcast(I32))


def tile_picked_ytani_act_p_kernel(
    tc, x_words, x_scales, w1, e_words, e_scales, qn, own, act, offs, refs, out
):
    nc = tc.nc
    with ExitStack() as ctx:
        keep = ctx.enter_context(tc.tile_pool(name="keep", bufs=1))
        late = ctx.enter_context(tc.tile_pool(name="late", bufs=1))
        psum = ctx.enter_context(tc.psum_pool(name="psum", bufs=1))

        def tile(name, shape, dtype, tag=None):
            return keep.tile(shape, dtype, name=name, tag=tag or name, align_bytes=64)

        offs_sb = keep.tile([P, S // 16], U16, name="offs_sb")
        refs_sb = keep.tile([P, V // 16], U16, name="refs_sb")
        xs_tab = tile("xs_tab", [P, T], U8)
        es_tab = tile("es_tab", [P, W], U8)
        qa_tab = late.tile([P, W], F32, name="qa_tab", offset=8192, align_bytes=64)
        xw_tab = tile("xw_tab", [P, T], U32)
        ew_tab = tile("ew_tab", [P, W], U32)
        w_cuts = (0, W_FIRST, P)
        w_raw = [tile("w_raw%d" % u, [P, PACK, PACK * (w_cuts[u + 1] - w_cuts[u])], F32) for u in range(2)]
        own_col = tile("own_col", [P, PACK], F32)
        ident = tile("ident", [P, P], F32)
        warm_in = tile("warm_in", [P, 1], F32)
        warm_out = tile("warm_out", [P, 1], F32)
        xs = tile("xs", [P, S], U8)
        es = tile("es", [P, V], U8)

        nc.gpsimd.memset(xs_tab[:].bitcast(I32), 0)
        nc.vector.memset(es_tab[:].bitcast(I32), 0)
        nc.vector.memset(warm_in[:], 0.0)
        nc.vector.memset(xs[:].bitcast(I32), 0)
        nc.vector.memset(es[:].bitcast(I32), 0)
        nc.vector.memset(qa_tab[:, 0:CLEAR_SPLIT], 0.0)
        make_identity(nc, ident[:])
        nc.scalar.activation(warm_out[:], warm_in[:], ACT.Abs_reciprocal_sqrt, bias=1.0)
        nc.scalar.copy(out=qa_tab[:, CLEAR_SPLIT:W], in_=warm_in[:].to_broadcast([P, W - CLEAR_SPLIT]))

        w_rows = w1.rearrange("(p r) c -> p r c", r=PACK)
        nc.sync.dma_start(out=w_raw[0][:], in_=w_rows[:, :, 0 : PACK * W_FIRST])
        nc.sync.dma_start(offs_sb[:], offs)
        nc.sync.dma_start(refs_sb[:], refs)
        load_scale_rows(nc, xs_tab, x_scales)
        nc.sync.dma_start(out=own_col[:], in_=own.rearrange("(p c) o -> p (c o)", c=PACK))
        load_scale_rows(nc, es_tab, e_scales)
        nc.sync.dma_start(out=w_raw[1][:], in_=w_rows[:, :, PACK * W_FIRST : H])
        nc.sync.dma_start(out=xw_tab[:].bitcast(I32), in_=x_words[0].rearrange("p n t -> p (n t)").bitcast(I32))

        xs_picked = tile("xs_picked", [P, S], U8)
        nc.vector.tensor_copy(xs_picked[:], xs_tab[:].indirect(offs_sb[:]))
        place_scale_rows(nc, xs, xs_picked)
        nc.sync.dma_start(out=qa_tab[QN_ROW : QN_ROW + 1, :], in_=qn[0:1, :])
        nc.sync.dma_start(out=qa_tab[ACT_ROW : ACT_ROW + 1, :], in_=act[0:1, :])
        nc.sync.dma_start(out=ew_tab[:].bitcast(I32), in_=e_words[0].rearrange("p n t -> p (n t)").bitcast(I32))
        es_picked = late.tile([P, 4 * HALF + 128], U8, name="es_picked", offset=4 * HALF - 64, align_bytes=64)
        nc.vector.tensor_copy(es_picked[:, 0:V], es_tab[:].indirect(refs_sb[:]))
        place_scale_rows(nc, es, es_picked)

        w_bf = tile("w_bf", [P, PACK, P, PACK], BF16)

        for copy, u, m0, m1 in ((nc.scalar.copy, 0, 0, W_FIRST), (nc.scalar.copy, 1, W_FIRST, W_SCALAR_END), (nc.vector.tensor_copy, 1, W_SCALAR_END, P)):
            copy(
                out=w_bf[:, :, m0:m1, :].rearrange("p j m r -> p m j r"),
                in_=w_raw[u][:, :, PACK * (m0 - w_cuts[u]) : PACK * (m1 - w_cuts[u])].rearrange("p r (m j) -> p m j r", j=PACK),
            )
        wq = tile("wq", [P, H], U32)
        ws = tile("ws", [P, H], U8)
        nc.vector.quantize_mx(out=wq[:].bitcast(FP8X4), scales=ws[:], in_=w_bf[:].rearrange("p j m r -> p (j m r)"))

        own_row = tile("own_row", [P, S], F32)
        own_ps = psum.tile([P, PACK, P], F32, name="own_ps", tag="s3")
        for c in range(PACK):
            nc.tensor.transpose(own_ps[:, c, :], own_col[:, c : c + 1].to_broadcast([P, P]), ident[:])
        nc.scalar.activation(
            own_row[:].rearrange("p (n c) -> p n c", c=PACK), own_ps[:].rearrange("p c n -> p n c"), ACT.Copy, scale=1.0 / Y_SCALE
        )

        x_cuts = ((0, P), (P, 2 * P), (2 * P, S))
        xq = []
        for i, (t0, t1) in enumerate(x_cuts):
            piece = tile("xq%d" % i, [P, t1 - t0], U32)
            nc.vector.tensor_copy(piece[:], xw_tab[:].indirect(offs_sb[:, t0 // 16 : t1 // 16]))
            xq += [piece[:, t - t0 : t - t0 + P] for t in range(t0, t1, P)]

        qa = [tile("qa%d" % g, [P, HALF], F32) for g in range(2)]
        for g in range(2):
            nc.scalar.activation(qa[g][:], qa_tab[:].indirect(refs_sb[:, 16 * g : 16 * (g + 1)]), ACT.Copy)

        h_first = [tile("h_bf0a", [P, P, PACK], BF16), late.tile([P, P, PACK], BF16, name="h_bf0b", offset=8192, align_bytes=64)]
        h_second = late.tile([P, HALF, PACK], BF16, name="h_bf1", offset=8192 + 1024, align_bytes=64)
        h_bf = [h_first[0][:], h_first[1][:], h_second[:, 0:P, :], h_second[:, P:HALF, :]]
        for c in range(NB):
            h_ps = psum.tile([P, PACK, P], F32, name="h_ps%d" % c, tag="h%d" % c)
            for j in range(PACK):
                nc.tensor.matmul_mx(
                    out=h_ps[:, j, :],
                    lhsT=wq[:, j * P : (j + 1) * P].bitcast(FP8X4),
                    lhsT_scale=ws[:, j * P : (j + 1) * P],
                    rhs=xq[c].bitcast(FP8X4),
                    rhs_scale=xs[:, c * P : (c + 1) * P],
                    start=True,
                    stop=True,
                )
            (nc.vector.tensor_copy if c == 0 else nc.scalar.copy)(out=h_bf[c], in_=h_ps[:].rearrange("p j n -> p n j"))

        nc.vector.tensor_copy(out=qa[0][P // 2 : P, :], in_=qa[1][0 : P // 2, :])
        qa_ps = psum.tile([P, 2, 2, P // 2], F32, name="qa_ps", tag="s2")
        for i in range(2):
            nc.tensor.transpose(qa_ps[:, i, :, :].rearrange("p g r -> p (g r)"), qa[0][:, i * P : (i + 1) * P], ident[:])
        qa_col = tile("qa_col", [P, NB, 2], F32)
        nc.scalar.activation(
            qa_col[:].rearrange("p (g i) r -> p i g r", g=2),
            qa_ps[:, :, :, QN_ROW : ACT_ROW + 1 : ACT_ROW - QN_ROW],
            ACT.Copy,
            scale=1.0 / Y_SCALE,
        )
        qn_own = {}
        for (u, b), successor in (((1, 2), "num0"),):
            qn_own[u, b] = tile("qn%d%d" % (u, b), [P, 1], F32, tag=successor)
            nc.scalar.activation(qn_own[u, b][:], qa_ps[:, b % 2, b // 2, QN_ROW : QN_ROW + 1], ACT.Copy, scale=1.0 / Y_SCALE)

        hq, hs, eq, s_ps, num = {}, {}, {}, {}, {}
        dneg_all = tile("dneg", [P, 2 * NB, HALF], F32)
        sgn_all = tile("sgn", [P, 2 * NB, HALF], F32)
        dneg = [dneg_all[:, u * NB : (u + 1) * NB, :] for u in range(2)]
        sgn = [sgn_all[:, u * NB : (u + 1) * NB, :] for u in range(2)]
        root = [tile("root%d" % u, [P, NB, HALF], F32) for u in range(2)]
        inv = {}

        def quantize_h(t0, values, words):
            hq[t0] = words
            hs[t0] = tile("hs%d" % t0, [P, values.shape[1]], U8)
            nc.vector.quantize_mx(out=words[:].bitcast(FP8X4), scales=hs[t0][:], in_=values.rearrange("p n j -> p (n j)"))

        def gather_e(g):
            pair = late.tile([P, HALF], U32, name="eq1", offset=4 * HALF, align_bytes=64) if g else tile("eq0", [P, HALF], U32)
            nc.vector.tensor_copy(pair[:], ew_tab[:].indirect(refs_sb[:, 16 * g : 16 * (g + 1)]))
            eq[2 * g], eq[2 * g + 1] = pair[:, 0:P], pair[:, P:HALF]

        def product(u, b):
            if u == 0:
                s_ps[b] = psum.tile([P, 2, HALF], F32, name="s_ps%d" % b, tag="s%d" % b)
            for t0, t1 in (((0, P), (P, HALF)), ((HALF, S),))[u]:
                nc.tensor.matmul_mx(
                    out=s_ps[b][:, u, t0 - u * HALF : t1 - u * HALF],
                    lhsT=eq[b].bitcast(FP8X4),
                    lhsT_scale=es[:, b * P : (b + 1) * P],
                    rhs=hq[t0][:].bitcast(FP8X4),
                    rhs_scale=hs[t0][:],
                    start=True,
                    stop=True,
                )

        def denominators(u, b):
            qn_col = qn_own[u, b][:] if (u, b) in qn_own else qa_col[:, b, 0:1]
            own_half = own_row[:, u * HALF : (u + 1) * HALF]
            nc.vector.scalar_tensor_tensor(dneg[u][:, b, :], s_ps[b][:, u, :], qn_col, own_half, ALU.subtract, ALU.subtract)

        def signs(i0, i1):
            nc.gpsimd.tensor_scalar(sgn_all[:, i0:i1, :], dneg_all[:, i0:i1, :], TINY, -TINY, ALU.min, ALU.max)

        def roots(u, b0, b1):
            nc.scalar.activation(root[u][:, b0:b1, :], dneg[u][:, b0:b1, :], ACT.Abs_reciprocal_sqrt)

        def roots_of(c, b0, b1):
            return root[c // 2][:, b0:b1, (c % 2) * P : (c % 2 + 1) * P]

        def squares(c, b0=0, b1=NB, on_vector=False):
            if b0 == 0:
                inv[c] = tile("inv%d" % c, [P, NB, P], F32)
            if on_vector:
                nc.vector.tensor_tensor(inv[c][:, b0:b1, :], roots_of(c, b0, b1), roots_of(c, b0, b1), ALU.mult)
            else:
                nc.scalar.activation(inv[c][:, b0:b1, :], roots_of(c, b0, b1), ACT.Square)

        def numerators(u, b0, b1):
            if b0 == 0:
                num[u] = tile("num%d" % u, [P, NB, HALF], F32)
            for b in range(b0, b1):
                nc.vector.scalar_tensor_tensor(num[u][:, b, :], s_ps[b][:, u, :], qa_col[:, b, 1:2], sgn[u][:, b, :], ALU.mult, ALU.mult)

        o_ps = {}

        def quotients(c, cuts, bank):
            u, cols = c // 2, slice((c % 2) * P, (c % 2 + 1) * P)
            first = cuts[0]
            o_ps[c, first] = psum.tile([P, (cuts[-1] - first) * P], F32, name="o_ps%d%d" % (c, first), tag=bank)
            for b0, b1 in zip(cuts, cuts[1:]):
                arg = tile("arg%d%d" % (c, b0), [P, b1 - b0, P], F32)
                nc.vector.tensor_tensor(arg[:], num[u][:, b0:b1, cols], inv[c][:, b0:b1, :], ALU.mult)
                for b in range(b0, b1):
                    nc.tensor.transpose(o_ps[c, first][:, (b - first) * P : (b - first + 1) * P], arg[:, b - b0, :], ident[:])

        def finish(c, b0, b1, queue):
            res = tile("res%d%d" % (c, b0), [P, (b1 - b0) * P], F32)
            nc.scalar.activation(res[:], o_ps[c, b0][:], ACT.Tanh, scale=-Y_SCALE / TINY)
            queue.dma_start(out=out[c * P : (c + 1) * P, b0 * P : b1 * P], in_=res[:])

        quantize_h(0, h_bf[0], late.tile([P, P], U32, name="hq0a", offset=8192 + 3072, align_bytes=64))
        gather_e(0)
        quantize_h(P, h_bf[1], late.tile([P, P], U32, name="hq0b", offset=4 * P, align_bytes=64))
        gather_e(1)
        hq[HALF] = late.tile([P, HALF], U32, name="hq1", offset=8 * HALF, align_bytes=64)
        hs[HALF] = tile("hs1", [P, HALF], U8)
        for i in range(2):
            cols = slice(i * P, (i + 1) * P)
            nc.vector.quantize_mx(out=hq[HALF][:, cols].bitcast(FP8X4), scales=hs[HALF][:, cols], in_=h_bf[2 + i].rearrange("p n j -> p (n j)"))
        for b in range(NB):
            product(0, b)
        for b in range(NB):
            denominators(0, b)
            product(1, b)
            roots(0, b, b + 1)
        for b in range(NB):
            denominators(1, b)
        for i0, i1 in ((0, 1), (1, 3), (3, 6), (6, 8)):
            signs(i0, i1)
        roots(1, 0, 1)
        squares(0)
        roots(1, 1, NB)
        squares(1)
        tanh_warm = tile("tanh_warm", [P, 1], F32)
        nc.scalar.activation(tanh_warm[:], root[1][:, NB - 1, 0:1], ACT.Tanh)
        squares(3)
        numerators(0, 0, NB)
        numerators(1, 0, 2)
        quotients(0, (0, NB), "h0")
        finish(0, 0, NB, nc.sync)
        quotients(1, (0, NB), "h1")
        numerators(1, 2, 3)
        squares(2, on_vector=True)
        finish(1, 0, NB, nc.sync)
        numerators(1, 3, NB)
        quotients(2, (0, 2), "h2")
        finish(2, 0, 2, nc.sync)
        quotients(2, (2, NB), "h3")
        finish(2, 2, NB, nc.sync)
        quotients(3, (0, 2), "s0")
        finish(3, 0, 2, nc.sync)
        quotients(3, (2, NB), "s1")
        finish(3, 2, NB, nc.scalar)
